import numpy as np
import ml_dtypes


def mxq(x, axis, fmt="e4m3"):
    dtype, down = {"e4m3": (ml_dtypes.float8_e4m3fn, 7), "e5m2": (ml_dtypes.float8_e5m2, 14)}[fmt]
    v = np.moveaxis(np.asarray(x, np.float32).astype(ml_dtypes.bfloat16).astype(np.float64), axis, -1)
    blocks = v.reshape(v.shape[:-1] + (-1, 32))
    amax = np.abs(blocks).max(-1, keepdims=True)
    byte = np.maximum(np.where(amax > 0, np.frexp(amax)[1] - 1 + 127, 0) - down, 1)
    scale = np.exp2(byte - 127.0)
    codes = (blocks / scale).astype(np.float32).astype(dtype).astype(np.float64)
    return np.moveaxis((codes * scale).reshape(v.shape), -1, axis)


WIDE = False


def mx_kscale(k):
    if not WIDE:
        return np.ones(k)
    levels = np.array([10, -10, 5, -5, 0])
    if k % 512:
        return np.exp2(np.random.permutation(np.resize(levels, k // 32))).repeat(32)
    a = np.empty((k // 512, 16))
    for p in range(k // 512):
        a[p, :8] = np.random.permutation(np.resize(levels, 8))
        for g in range(8):
            far = levels[np.abs(levels - a[p, g]) >= 10]
            a[p, g + 8] = far[np.random.randint(len(far))]
    return np.exp2(a.ravel()).repeat(32)


def f64(x):
    return np.asarray(x).astype(np.float64)


def striped(idx):
    return np.tile(idx.reshape(-1, 16).T, (8, 1)).astype(np.uint16)


def unstriped(offs):
    return offs[:16].T.reshape(-1).astype(np.int64)


E2M1 = np.array([0.0, 0.5, 1.0, 1.5, 2.0, 3.0, 4.0, 6.0, -0.0, -0.5, -1.0, -1.5, -2.0, -3.0, -4.0, -6.0])


def pack_weight(w, fmt):
    k, n = w.shape
    w = f64(np.asarray(w, np.float32).astype(ml_dtypes.bfloat16)).reshape(k // 32, 32, n)
    amax = np.abs(w).max(1)
    if fmt == "e4m3":
        byte = np.frexp(amax)[1] - 1 + 127 - 7
    else:
        mant, ex = np.frexp(amax / 6.0)
        byte = np.where(mant > 0.5, ex, ex - 1) + 127
    byte = np.clip(np.where(amax > 0, byte, 1), 1, 254)
    scaled = (w * np.exp2(127.0 - byte)[:, None, :]).reshape(k, n).astype(np.float32)
    by_word = np.ascontiguousarray(scaled.reshape(k // 512, 128, 4, n).transpose(0, 1, 3, 2))
    if fmt == "e4m3":
        words = by_word.astype(ml_dtypes.float8_e4m3fn).view(np.uint8)
    else:
        c = by_word.astype(ml_dtypes.float4_e2m1fn).view(np.uint8) & 0xF
        words = (c[..., 0::2] | (c[..., 1::2] << 4)).reshape(k // 512, 128, 2 * n)
    return np.ascontiguousarray(words), np.ascontiguousarray(byte.astype(np.uint8).reshape(k // 512, 16, n))


def unpack_weight(words, scales, fmt):
    g, _, n = scales.shape
    words = np.ascontiguousarray(words).reshape(g, 128, n, -1)
    if fmt == "e4m3":
        vals = words.view(ml_dtypes.float8_e4m3fn).astype(np.float64)
    else:
        nib = np.empty((g, 128, n, 4), np.uint8)
        nib[..., 0::2] = words & 0xF
        nib[..., 1::2] = words >> 4
        vals = E2M1[nib]
    vals = vals * np.repeat(np.exp2(scales.astype(np.float64) - 127.0), 8, axis=1)[..., None]
    return vals.transpose(0, 1, 3, 2).reshape(g * 512, n)


def gelu(v):
    return 0.5 * v * (1.0 + np.tanh(np.sqrt(2.0 / np.pi) * (v + 0.044715 * v**3)))


def often(T, S):
    return np.random.permutation(T)[(T * np.random.uniform(0, 1, S) ** 4).astype(np.int64)]


K, H, N, T, S, T2, P = 512, 1024, 512, 2048, 1024, 2048, 512

def setup_inputs():
    n = np.random.standard_normal
    s = mx_kscale(K)[:, None]
    u = mx_kscale(H)[:, None]
    tab_words, tab_scales = pack_weight(n((K, T)) * s, "e4m3")
    tab2_words, tab2_scales = pack_weight(n((K, T2)) * s, "e4m3")
    w4_words, w4_scales = pack_weight(0.7 * n((K, H)) / np.sqrt(K) / s, "e2m1")
    w8_words, w8_scales = pack_weight(n((K, H)) / np.sqrt(K) / s, "e4m3")
    return {
        "tab_words": tab_words, "tab_scales": tab_scales,
        "tab2_words": tab2_words, "tab2_scales": tab2_scales,
        "offs": striped(np.random.permutation(T)[:S]),
        "pos1": striped(often(S, P)),
        "offs2": striped(np.random.permutation(T2)[:P]),
        "ws": (0.5 * n((K, H)) / np.sqrt(K) / s).astype(np.float32),
        "bs": (1.0 + 0.2 * n(H)).astype(np.float32),
        "w4_words": w4_words, "w4_scales": w4_scales,
        "w8_words": w8_words, "w8_scales": w8_scales,
        "gain": (np.random.uniform(0.5, 2.0, H) * u[:, 0]).astype(np.float32),
        "wo": (n((H, N)) / np.sqrt(H) / u).astype(np.float32),
        "bo": (0.3 * n(N)).astype(np.float32),
    }

def reference(tab_words, tab_scales, tab2_words, tab2_scales, offs, pos1, offs2, ws, bs,
              w4_words, w4_scales, w8_words, w8_scales, gain, wo, bo):
    v = unpack_weight(tab_words, tab_scales, "e4m3")[:, unstriped(offs)]
    v2 = unpack_weight(tab2_words, tab2_scales, "e4m3")[:, unstriped(offs2)]
    x1 = (mxq(f64(ws), 0, "e4m3").T @ v) + f64(bs)[:, None]
    x2 = unpack_weight(w4_words, w4_scales, "e2m1").T @ v
    b = unpack_weight(w8_words, w8_scales, "e4m3").T @ v2
    z = np.tanh(x1[:, unstriped(pos1)] * b + x2[:, unstriped(pos1)]) * f64(gain)[:, None]
    return (mxq(f64(wo), 0, "e4m3").T @ mxq(z, 0, "e4m3")) + f64(bo)[:, None]

@@ -1,0 +1,275 @@
+from contextlib import ExitStack
+
+import concourse.mybir as mybir
+from concourse.masks import make_identity
+
+K, H, N, T, S, T2, J = 512, 1024, 512, 2048, 1024, 2048, 512
+FLOPS = 2 * K * H * S * 2 + 2 * K * H * J + 2 * H * N * J
+
+F32 = mybir.dt.float32
+BF16 = mybir.dt.bfloat16
+I32 = mybir.dt.int32
+U32 = mybir.dt.uint32
+U16 = mybir.dt.uint16
+U8 = mybir.dt.uint8
+FP8X4 = mybir.dt.float8_e4m3fn_x4
+FP4X4 = mybir.dt.float4_e2m1fn_x4
+ACT = mybir.ActivationFunctionType
+ALU = mybir.AluOpType
+
+P = 128
+BANK = 512
+SLICES = H // P
+PASSES = H // 512
+TAIL = [(0, 256), (256, 512)]
+
+
+def tile_list_lint_autofix_edits_kernel(
+    tc, tab_words, tab_scales, tab2_words, tab2_scales, offs, pos1, offs2, ws, bs,
+    w4_words, w4_scales, w8_words, w8_scales, gain, wo, bo, out,
+):
+    nc = tc.nc
+    with ExitStack() as ctx:
+        held = ctx.enter_context(tc.tile_pool(name="held", bufs=1))
+        ring = ctx.enter_context(tc.tile_pool(name="ring", bufs=2))
+        psum = ctx.enter_context(tc.psum_pool(name="psum", bufs=4))
+
+        def keep(shape, dtype, name):
+            return held.tile(shape, dtype, name=name, align_bytes=64)
+
+        def load_plane(queue, plane, rows):
+            for q in range(4):
+                queue.dma_start(out=plane[32 * q : 32 * q + 4, :].bitcast(I32), in_=rows[0, 4 * q : 4 * q + 4, :].bitcast(I32))
+
+        offs_t = held.tile([P, S // 16], U16, name="offs_t")
+        pos_t = held.tile([P, J // 16], U16, name="pos_t")
+        offs2_t = held.tile([P, J // 16], U16, name="offs2_t")
+        tab_w = keep([P, T], U32, "tab_w")
+        tab_s = keep([P, T], U8, "tab_s")
+        tab2_s = keep([P, T2], U8, "tab2_s")
+        w4_w_raw = keep([P, 2 * H], U8, "w4_w_raw")
+        w4_s_raw = keep([P, H], U8, "w4_s_raw")
+        w8_s_raw = keep([P, H], U8, "w8_s_raw")
+
+        nc.vector.memset(tab_s[:].bitcast(I32), 0)
+        nc.vector.memset(w4_s_raw[:].bitcast(I32), 0)
+        nc.gpsimd.memset(tab2_s[:].bitcast(I32), 0)
+        nc.gpsimd.memset(w8_s_raw[:].bitcast(I32), 0)
+        rows = [keep([P, 2 * P], F32, f"rows{e}") for e in range(2)]
+        ident = keep([P, P], F32, "ident")
+        nc.gpsimd.memset(rows[0][:], 0.0)
+        make_identity(nc, ident[:])
+        with tc.tile_pool(name="first", bufs=1) as first:
+            warm = first.tile([P, 8], F32, name="warm")
+            nc.vector.memset(warm[:], 0.0)
+            nc.scalar.activation(out=warm[:, 0:1], in_=warm[:, 1:2], func=ACT.Tanh)
+        later = ctx.enter_context(tc.tile_pool(name="later", bufs=1))
+
+        ws_rows = ws.rearrange("(p j) r -> p j r", j=4)
+        ws_raw = [later.tile([P, 4, 256], F32, name=f"ws_raw{c}") for c in range(4)]
+        wo_raw = [later.tile([P, 4, N], F32, name=f"wo_raw{a}") for a in range(PASSES)]
+        tab2_w = later.tile([P, T2], U32, name="tab2_w")
+        w8_w_raw = later.tile([P, H], I32, name="w8_w_raw")
+
+        def plane_rows(plane, rows, q):
+            nc.sync.dma_start(out=plane[32 * q : 32 * q + 4, :].bitcast(I32), in_=rows[0, 4 * q : 4 * q + 4, :].bitcast(I32))
+
+        by_slot = "(g t i) -> t g i"
+        nc.sync.dma_start(offs_t[:], offs)
+        nc.sync.dma_start(offs2_t[:], offs2)
+        nc.sync.dma_start(out=tab_w[:].bitcast(I32), in_=tab_words[0].rearrange("p t i -> p (t i)").bitcast(I32))
+        nc.sync.dma_start(pos_t[:], pos1)
+        nc.sync.dma_start(out=w4_w_raw[:].bitcast(I32), in_=w4_words[0].bitcast(I32))
+        load_plane(nc.sync, tab_s, tab_scales)
+        nc.sync.dma_start(out=ws_raw[0][:], in_=ws_rows[:, :, 0:256])
+        load_plane(nc.sync, w4_s_raw, w4_scales)
+        nc.sync.dma_start(out=ws_raw[1][:], in_=ws_rows[:, :, 256:512])
+        nc.sync.dma_start(out=rows[0][0:4, :].rearrange("t (g i) -> t g i", i=8), in_=bs.rearrange(by_slot, t=4, i=8))
+        plane_rows(tab2_s, tab2_scales, 0)
+        plane_rows(tab2_s, tab2_scales, 1)
+        nc.sync.dma_start(out=tab2_w[:].bitcast(I32), in_=tab2_words[0].rearrange("p t i -> p (t i)").bitcast(I32))
+        plane_rows(tab2_s, tab2_scales, 2)
+        plane_rows(tab2_s, tab2_scales, 3)
+        nc.sync.dma_start(out=w8_w_raw[:], in_=w8_words[0].rearrange("p c i -> p (c i)").bitcast(I32))
+        load_plane(nc.sync, w8_s_raw, w8_scales)
+        nc.sync.dma_start(out=ws_raw[2][:], in_=ws_rows[:, :, 512:768])
+        nc.sync.dma_start(out=ws_raw[3][:], in_=ws_rows[:, :, 768:1024])
+        wo_rows = wo.rearrange("(a q t i) n -> a t q i n", a=PASSES, t=4, i=8)
+        for a in range(PASSES):
+            for t in range(4):
+                nc.sync.dma_start(out=wo_raw[a][:, t, :], in_=wo_rows[a, t])
+        nc.gpsimd.memset(rows[1][:], 0.0)
+        nc.sync.dma_start(out=rows[1][0:4, :].rearrange("t (g i) -> t g i", i=8), in_=gain.rearrange(by_slot, t=4, i=8))
+        nc.sync.dma_start(out=rows[1][4:8, 0:P], in_=bo.rearrange("(b p) -> b p", p=P))
+
+        def onto_partitions(staged, name):
+            turned = psum.tile([P, BANK], F32, name="work")
+            for a in range(PASSES):
+                nc.tensor.transpose(turned[:, P * a : P * (a + 1)], staged[:, P * a : P * (a + 1)], ident[:])
+            cols = keep([P, PASSES, 8], F32, name)
+            nc.vector.tensor_copy(out=cols[:], in_=turned[:, 0 : 2 * P].rearrange("p (a c) -> p a c", a=PASSES)[:, :, 0:8])
+            return cols
+
+        bs_cols = onto_partitions(rows[0], "bs_cols")
+
+        v_w = [keep([P, BANK], U32, f"v_w{h}") for h in range(2)]
+        v_s = [keep([P, BANK], U8, f"v_s{h}") for h in range(2)]
+        v2_w = keep([P, J], U32, "v2_w")
+        v2_s = keep([P, J], U8, "v2_s")
+        w4_w = keep([P, 2 * H], U8, "w4_w")
+        w4_s = keep([P, H], U8, "w4_s")
+        w8_w = keep([P, H], I32, "w8_w")
+        w8_s = keep([P, H], U8, "w8_s")
+        ws_b = [keep([P, 4 * 512], BF16, f"ws_b{a}") for a in range(PASSES)]
+        ws_w = [keep([P, 512], U32, f"ws_w{a}") for a in range(PASSES)]
+        ws_s = [keep([P, 512], U8, f"ws_s{a}") for a in range(PASSES)]
+
+        def reorder(dst, src):
+            nc.vector.tensor_copy(
+                out=dst.rearrange("p (a t q i) -> p a q t i", a=PASSES, t=4, q=16),
+                in_=src.rearrange("p (a q t i) -> p a q t i", a=PASSES, t=4, q=16),
+            )
+
+        def round_ws(c):
+            a, half = divmod(c, 2)
+            dst = ws_b[a][:].rearrange("p (t q i j) -> p q t j i", t=4, q=16, j=4)[:, 8 * half : 8 * half + 8]
+            nc.scalar.copy(out=dst, in_=ws_raw[c][:].rearrange("p j (q t i) -> p q t j i", t=4, i=8))
+
+        def quantize(words, plane, src):
+            nc.vector.quantize_mx(out=words[:].bitcast(FP8X4), scales=plane[:], in_=src[:])
+
+        round_ws(0)
+        round_ws(1)
+        for h in range(2):
+            nc.vector.tensor_copy(out=v_w[h][:], in_=tab_w[:].indirect(offs_t[:, 32 * h : 32 * (h + 1)]))
+        reorder(w4_w[:].bitcast(I32), w4_w_raw[:].bitcast(I32))
+        nc.vector.tensor_copy(out=v_s[0][:], in_=tab_s[:].indirect(offs_t[:, 0:32]))
+        reorder(w4_s[:].bitcast(I32), w4_s_raw[:].bitcast(I32))
+        nc.vector.tensor_copy(out=v_s[1][:], in_=tab_s[:].indirect(offs_t[:, 32:64]))
+        quantize(ws_w[0], ws_s[0], ws_b[0])
+        nc.vector.tensor_copy(out=v2_s[:], in_=tab2_s[:].indirect(offs2_t[:]))
+        nc.vector.tensor_copy(out=v2_w[:], in_=tab2_w[:].indirect(offs2_t[:]))
+        reorder(w8_w[:], w8_w_raw[:])
+        reorder(w8_s[:].bitcast(I32), w8_s_raw[:].bitcast(I32))
+
+        x1 = [keep([P, S], F32, f"x1_{s}") for s in range(SLICES)]
+        x2 = [keep([P, S], F32, f"x2_{s}") for s in range(SLICES)]
+        b = [keep([P, J], F32, f"b_{s}") for s in range(SLICES)]
+        u = [keep([P, 4, J], F32, f"u_{a}") for a in range(PASSES)]
+
+        def product(lhsT, lhsT_scale, words, plane):
+            bank = psum.tile([P, BANK], F32, name="work")
+            nc.tensor.matmul_mx(out=bank[:], lhsT=lhsT, lhsT_scale=lhsT_scale, rhs=words[:].bitcast(FP8X4), rhs_scale=plane[:], start=True, stop=True)
+            return bank
+
+        def first_stage(s):
+            a, t = divmod(s, 4)
+            cols = slice(P * s, P * (s + 1))
+            in_pass = slice(P * t, P * (t + 1))
+            for h in range(2):
+                bank = product(ws_w[a][:, in_pass].bitcast(FP8X4), ws_s[a][:, in_pass], v_w[h], v_s[h])
+                nc.scalar.activation(out=x1[s][:, BANK * h : BANK * (h + 1)], in_=bank[:], func=ACT.Identity, bias=bs_cols[:, a, t : t + 1])
+            bank = product(w8_w[:, cols].bitcast(FP8X4), w8_s[:, cols], v2_w, v2_s)
+            nc.scalar.copy(out=b[s][:], in_=bank[:])
+            for h in range(2):
+                bank = product(w4_w[:, 2 * P * s : 2 * P * (s + 1)].bitcast(FP4X4), w4_s[:, cols], v_w[h], v_s[h])
+                nc.scalar.copy(out=x2[s][:, BANK * h : BANK * (h + 1)], in_=bank[:])
+
+        def combine(s, j0, j1):
+            a, t = divmod(s, 4)
+            picks = pos_t[:, j0 // 16 : j1 // 16]
+            scaled = ring.tile([P, J], F32, name="scaled")
+            nc.vector.tensor_tensor(scaled[:, j0:j1], x1[s][:].indirect(picks), b[s][:, j0:j1], ALU.mult)
+            nc.vector.tensor_tensor(u[a][:, t, j0:j1], x2[s][:].indirect(picks), scaled[:, j0:j1], ALU.add)
+
+        def tanh(s, j0, j1):
+            a, t = divmod(s, 4)
+            nc.scalar.activation(out=u[a][:, t, j0:j1], in_=u[a][:, t, j0:j1], func=ACT.Tanh)
+
+        def make_z(a, j0, j1):
+            width = j1 - j0
+            z_b = keep([P, 4 * width], BF16, f"z_b{a}_{j0}")
+            z_w = keep([P, width], U32, f"z_w{a}_{j0}")
+            z_s = keep([P, width], U8, f"z_s{a}_{j0}")
+            nc.vector.tensor_tensor(
+                z_b[:].rearrange("p (c i t) -> p c t i", t=4, i=4),
+                u[a][:, :, j0:j1].rearrange("p t (c i) -> p c t i", i=4),
+                late_cols[:, a, 0:4].unsqueeze(1).unsqueeze(3).to_broadcast([P, width // 4, 4, 4]),
+                ALU.mult,
+            )
+            quantize(z_w, z_s, z_b)
+            return z_w, z_s
+
+        wo_b = [keep([P, 4 * N], BF16, f"wo_b{a}") for a in range(PASSES)]
+        wo_w = [keep([P, N], U32, f"wo_w{a}") for a in range(PASSES)]
+        wo_s = [keep([P, N], U8, f"wo_s{a}") for a in range(PASSES)]
+
+        def make_wo(a):
+            nc.vector.tensor_copy(
+                out=wo_b[a][:].rearrange("p (c i t) -> p c t i", t=4, i=4),
+                in_=wo_raw[a][:].rearrange("p t (c i) -> p c t i", i=4),
+            )
+            quantize(wo_w[a], wo_s[a], wo_b[a])
+
+        def second_pass(acc, a, nt, words, plane):
+            cols = slice(P * nt, P * (nt + 1))
+            nc.tensor.matmul_mx(out=acc, lhsT=wo_w[a][:, cols].bitcast(FP8X4), lhsT_scale=wo_s[a][:, cols], rhs=words.bitcast(FP8X4), rhs_scale=plane, start=(a == 0), stop=(a == PASSES - 1))
+
+        out_rows = out.rearrange("(b p) j -> p b j", p=P)
+
+        def finish(acc, res, nt, on_scalar):
+            if on_scalar:
+                nc.scalar.activation(out=res, in_=acc, func=ACT.Identity, bias=late_cols[:, 0, 4 + nt : 5 + nt])
+            else:
+                nc.vector.tensor_scalar(res, acc, late_cols[:, 0, 4 + nt : 5 + nt], None, ALU.add)
+
+        z0 = None
+        late_cols = None
+        for s in range(SLICES):
+            first_stage(s)
+            if s == 1:
+                round_ws(2)
+                round_ws(3)
+                quantize(ws_w[1], ws_s[1], ws_b[1])
+            if s < SLICES - 1:
+                combine(s, 0, J)
+            if s == 2 or s == 3:
+                make_wo(s - 2)
+            if s == 4:
+                late_cols = onto_partitions(rows[1], "late_cols")
+            if s >= 2:
+                tanh(s - 2, 0, J)
+            if s == 5:
+                z0 = make_z(0, 0, J)
+        tanh(SLICES - 2, 0, J)
+
+        (a0, a1), (b0, b1) = TAIL
+        last = [psum.tile([P, BANK], F32, name="last") for nt in range(4)]
+        for nt in range(4):
+            second_pass(last[nt][:, 0 : b1 - b0], 0, nt, z0[0][:, b0:b1], z0[1][:, b0:b1])
+
+        combine(SLICES - 1, a0, a1)
+        tanh(SLICES - 1, a0, a1)
+        combine(SLICES - 1, b0, b1)
+        tanh(SLICES - 1, b0, b1)
+        z1 = make_z(1, a0, a1)
+        z2 = make_z(1, b0, b1)
+        for pair in range(2):
+            bank = psum.tile([P, BANK], F32, name="work")
+            res = keep([P, 2, a1 - a0], F32, f"res_a{pair}")
+            for e in range(2):
+                nt = 2 * pair + e
+                acc = bank[:, 256 * e : 256 * e + a1 - a0]
+                second_pass(acc, 0, nt, z0[0][:, a0:a1], z0[1][:, a0:a1])
+                second_pass(acc, 1, nt, z1[0][:], z1[1][:])
+            for e in range(2):
+                finish(bank[:, 256 * e : 256 * e + a1 - a0], res[:, e, :], 2 * pair + e, True)
+            nc.sync.dma_start(out=out_rows[:, 2 * pair : 2 * pair + 2, a0:a1], in_=res[:])
+        for nt in range(4):
+            second_pass(last[nt][:, 0 : b1 - b0], 1, nt, z2[0][:], z2[1][:])
+        for pair in range(2):
+            res = keep([P, 2, b1 - b0], F32, f"res_b{pair}")
+            for e in range(2):
+                nt = 2 * pair + e
+                finish(last[nt][:, 0 : b1 - b0], res[:, e, :], nt, e == 0)
+            nc.sync.dma_start(out=out_rows[:, 2 * pair : 2 * pair + 2, b0:b1], in_=res[:])

@@ -39,7 +39,7 @@ def tile_list_lint_autofix_edits_kernel(
 
         def load_plane(queue, plane, rows):
             for q in range(4):
-                queue.dma_start(out=plane[32 * q : 32 * q + 4, :].bitcast(I32), in_=rows[0, 4 * q : 4 * q + 4, :].bitcast(I32))
+                queue.dma_start(out=plane[32 * q : 32 * q + 4].bitcast(I32), in_=rows[0, 4 * q : 4 * q + 4, :].bitcast(I32))
 
         offs_t = held.tile([P, S // 16], U16, name="offs_t")
         pos_t = held.tile([P, J // 16], U16, name="pos_t")
@@ -47,18 +47,16 @@ def tile_list_lint_autofix_edits_kernel(
         tab_w = keep([P, T], U32, "tab_w")
         tab_s = keep([P, T], U8, "tab_s")
         tab2_s = keep([P, T2], U8, "tab2_s")
-        w4_w_raw = keep([P, 2 * H], U8, "w4_w_raw")
-        w4_s_raw = keep([P, H], U8, "w4_s_raw")
-        w8_s_raw = keep([P, H], U8, "w8_s_raw")
+        w_s_raw = keep([P, 2 * H], U8, "w_s_raw")
 
         nc.vector.memset(tab_s[:].bitcast(I32), 0)
-        nc.vector.memset(w4_s_raw[:].bitcast(I32), 0)
-        nc.gpsimd.memset(tab2_s[:].bitcast(I32), 0)
-        nc.gpsimd.memset(w8_s_raw[:].bitcast(I32), 0)
+        nc.vector.memset(tab2_s[:].bitcast(I32), 0)
+        nc.vector.memset(w_s_raw[:].bitcast(I32), 0)
         rows = [keep([P, 2 * P], F32, f"rows{e}") for e in range(2)]
         ident = keep([P, P], F32, "ident")
-        nc.gpsimd.memset(rows[0][:], 0.0)
+        nc.vector.memset(rows[0][:], 0.0)
         make_identity(nc, ident[:])
+        load_plane(nc.gpsimd, tab2_s[:], tab2_scales)
         with tc.tile_pool(name="first", bufs=1) as first:
             warm = first.tile([P, 8], F32, name="warm")
             nc.vector.memset(warm[:], 0.0)
@@ -66,39 +64,31 @@ def tile_list_lint_autofix_edits_kernel(
         later = ctx.enter_context(tc.tile_pool(name="later", bufs=1))
 
         ws_rows = ws.rearrange("(p j) r -> p j r", j=4)
-        ws_raw = [later.tile([P, 4, 256], F32, name=f"ws_raw{c}") for c in range(4)]
+        ws_raw = [keep([P, 4, 512], F32, "ws_raw0"), later.tile([P, 4, 512], F32, name="ws_raw1")]
         wo_raw = [later.tile([P, 4, N], F32, name=f"wo_raw{a}") for a in range(PASSES)]
         tab2_w = later.tile([P, T2], U32, name="tab2_w")
         w8_w_raw = later.tile([P, H], I32, name="w8_w_raw")
-
-        def plane_rows(plane, rows, q):
-            nc.sync.dma_start(out=plane[32 * q : 32 * q + 4, :].bitcast(I32), in_=rows[0, 4 * q : 4 * q + 4, :].bitcast(I32))
+        w4_w_raw = later.tile([P, 2 * H], U8, name="w4_w_raw")
 
         by_slot = "(g t i) -> t g i"
         nc.sync.dma_start(offs_t[:], offs)
         nc.sync.dma_start(offs2_t[:], offs2)
-        nc.sync.dma_start(out=tab_w[:].bitcast(I32), in_=tab_words[0].rearrange("p t i -> p (t i)").bitcast(I32))
         nc.sync.dma_start(pos_t[:], pos1)
-        nc.sync.dma_start(out=w4_w_raw[:].bitcast(I32), in_=w4_words[0].bitcast(I32))
-        load_plane(nc.sync, tab_s, tab_scales)
-        nc.sync.dma_start(out=ws_raw[0][:], in_=ws_rows[:, :, 0:256])
-        load_plane(nc.sync, w4_s_raw, w4_scales)
-        nc.sync.dma_start(out=ws_raw[1][:], in_=ws_rows[:, :, 256:512])
+        nc.sync.dma_start(out=tab_w[:].bitcast(I32), in_=tab_words[0].rearrange("p t i -> p (t i)").bitcast(I32))
+        nc.sync.dma_start(out=ws_raw[0][:], in_=ws_rows[:, :, 0:512])
+        load_plane(nc.sync, tab_s[:], tab_scales)
+        nc.sync.dma_start(out=ws_raw[1][:], in_=ws_rows[:, :, 512:1024])
         nc.sync.dma_start(out=rows[0][0:4, :].rearrange("t (g i) -> t g i", i=8), in_=bs.rearrange(by_slot, t=4, i=8))
-        plane_rows(tab2_s, tab2_scales, 0)
-        plane_rows(tab2_s, tab2_scales, 1)
+        load_plane(nc.sync, w_s_raw[:, H : 2 * H], w8_scales)
         nc.sync.dma_start(out=tab2_w[:].bitcast(I32), in_=tab2_words[0].rearrange("p t i -> p (t i)").bitcast(I32))
-        plane_rows(tab2_s, tab2_scales, 2)
-        plane_rows(tab2_s, tab2_scales, 3)
         nc.sync.dma_start(out=w8_w_raw[:], in_=w8_words[0].rearrange("p c i -> p (c i)").bitcast(I32))
-        load_plane(nc.sync, w8_s_raw, w8_scales)
-        nc.sync.dma_start(out=ws_raw[2][:], in_=ws_rows[:, :, 512:768])
-        nc.sync.dma_start(out=ws_raw[3][:], in_=ws_rows[:, :, 768:1024])
+        load_plane(nc.sync, w_s_raw[:, 0:H], w4_scales)
+        nc.sync.dma_start(out=w4_w_raw[:].bitcast(I32), in_=w4_words[0].bitcast(I32))
         wo_rows = wo.rearrange("(a q t i) n -> a t q i n", a=PASSES, t=4, i=8)
         for a in range(PASSES):
             for t in range(4):
                 nc.sync.dma_start(out=wo_raw[a][:, t, :], in_=wo_rows[a, t])
-        nc.gpsimd.memset(rows[1][:], 0.0)
+        nc.vector.memset(rows[1][:], 0.0)
         nc.sync.dma_start(out=rows[1][0:4, :].rearrange("t (g i) -> t g i", i=8), in_=gain.rearrange(by_slot, t=4, i=8))
         nc.sync.dma_start(out=rows[1][4:8, 0:P], in_=bo.rearrange("(b p) -> b p", p=P))
 
@@ -107,7 +97,7 @@ def tile_list_lint_autofix_edits_kernel(
             for a in range(PASSES):
                 nc.tensor.transpose(turned[:, P * a : P * (a + 1)], staged[:, P * a : P * (a + 1)], ident[:])
             cols = keep([P, PASSES, 8], F32, name)
-            nc.vector.tensor_copy(out=cols[:], in_=turned[:, 0 : 2 * P].rearrange("p (a c) -> p a c", a=PASSES)[:, :, 0:8])
+            nc.scalar.copy(out=cols[:], in_=turned[:, 0 : 2 * P].rearrange("p (a c) -> p a c", a=PASSES)[:, :, 0:8])
             return cols
 
         bs_cols = onto_partitions(rows[0], "bs_cols")
@@ -117,44 +107,47 @@ def tile_list_lint_autofix_edits_kernel(
         v2_w = keep([P, J], U32, "v2_w")
         v2_s = keep([P, J], U8, "v2_s")
         w4_w = keep([P, 2 * H], U8, "w4_w")
-        w4_s = keep([P, H], U8, "w4_s")
+        w_s = keep([P, 2 * H], U8, "w_s")
         w8_w = keep([P, H], I32, "w8_w")
-        w8_s = keep([P, H], U8, "w8_s")
         ws_b = [keep([P, 4 * 512], BF16, f"ws_b{a}") for a in range(PASSES)]
-        ws_w = [keep([P, 512], U32, f"ws_w{a}") for a in range(PASSES)]
-        ws_s = [keep([P, 512], U8, f"ws_s{a}") for a in range(PASSES)]
+        ws_w = keep([P, H], U32, "ws_w")
+        ws_s = keep([P, H], U8, "ws_s")
 
-        def reorder(dst, src):
+        def reorder(dst, src, groups):
             nc.vector.tensor_copy(
-                out=dst.rearrange("p (a t q i) -> p a q t i", a=PASSES, t=4, q=16),
-                in_=src.rearrange("p (a q t i) -> p a q t i", a=PASSES, t=4, q=16),
+                out=dst.rearrange("p (a t q i) -> p a q t i", a=groups, t=4, q=16),
+                in_=src.rearrange("p (a q t i) -> p a q t i", a=groups, t=4, q=16),
             )
 
-        def round_ws(c):
-            a, half = divmod(c, 2)
-            dst = ws_b[a][:].rearrange("p (t q i j) -> p q t j i", t=4, q=16, j=4)[:, 8 * half : 8 * half + 8]
-            nc.scalar.copy(out=dst, in_=ws_raw[c][:].rearrange("p j (q t i) -> p q t j i", t=4, i=8))
+        def round_ws(s):
+            a, t = divmod(s, 4)
+            nc.scalar.copy(
+                out=ws_b[a][:, 512 * t : 512 * (t + 1)].rearrange("p (q i e j) -> p q i j e", q=16, e=2, j=4),
+                in_=ws_raw[a][:].rearrange("p j (q t i e) -> p t q i j e", t=4, i=4, e=2)[:, t],
+            )
 
         def quantize(words, plane, src):
-            nc.vector.quantize_mx(out=words[:].bitcast(FP8X4), scales=plane[:], in_=src[:])
+            nc.vector.quantize_mx(out=words.bitcast(FP8X4), scales=plane, in_=src)
 
-        round_ws(0)
-        round_ws(1)
+        for s in range(SLICES):
+            round_ws(s)
         for h in range(2):
             nc.vector.tensor_copy(out=v_w[h][:], in_=tab_w[:].indirect(offs_t[:, 32 * h : 32 * (h + 1)]))
-        reorder(w4_w[:].bitcast(I32), w4_w_raw[:].bitcast(I32))
-        nc.vector.tensor_copy(out=v_s[0][:], in_=tab_s[:].indirect(offs_t[:, 0:32]))
-        reorder(w4_s[:].bitcast(I32), w4_s_raw[:].bitcast(I32))
-        nc.vector.tensor_copy(out=v_s[1][:], in_=tab_s[:].indirect(offs_t[:, 32:64]))
-        quantize(ws_w[0], ws_s[0], ws_b[0])
+        for h in range(2):
+            nc.vector.tensor_copy(out=v_s[h][:], in_=tab_s[:].indirect(offs_t[:, 32 * h : 32 * (h + 1)]))
+        for half in range(2):
+            quantize(ws_w[:, 256 * half : 256 * (half + 1)], ws_s[:, 256 * half : 256 * (half + 1)], ws_b[0][:, 1024 * half : 1024 * (half + 1)])
         nc.vector.tensor_copy(out=v2_s[:], in_=tab2_s[:].indirect(offs2_t[:]))
         nc.vector.tensor_copy(out=v2_w[:], in_=tab2_w[:].indirect(offs2_t[:]))
-        reorder(w8_w[:], w8_w_raw[:])
-        reorder(w8_s[:].bitcast(I32), w8_s_raw[:].bitcast(I32))
+        reorder(w8_w[:], w8_w_raw[:], PASSES)
+        reorder(w_s[:].bitcast(I32), w_s_raw[:].bitcast(I32), 2 * PASSES)
+        reorder(w4_w[:].bitcast(I32), w4_w_raw[:].bitcast(I32), PASSES)
+        quantize(ws_w[:, 512:1024], ws_s[:, 512:1024], ws_b[1][:])
 
         x1 = [keep([P, S], F32, f"x1_{s}") for s in range(SLICES)]
         x2 = [keep([P, S], F32, f"x2_{s}") for s in range(SLICES)]
         b = [keep([P, J], F32, f"b_{s}") for s in range(SLICES)]
+        scaled = {}
         u = [keep([P, 4, J], F32, f"u_{a}") for a in range(PASSES)]
 
         def product(lhsT, lhsT_scale, words, plane):
@@ -162,25 +155,24 @@ def tile_list_lint_autofix_edits_kernel(
             nc.tensor.matmul_mx(out=bank[:], lhsT=lhsT, lhsT_scale=lhsT_scale, rhs=words[:].bitcast(FP8X4), rhs_scale=plane[:], start=True, stop=True)
             return bank
 
-        def first_stage(s):
+        def scale_side(s):
             a, t = divmod(s, 4)
             cols = slice(P * s, P * (s + 1))
-            in_pass = slice(P * t, P * (t + 1))
             for h in range(2):
-                bank = product(ws_w[a][:, in_pass].bitcast(FP8X4), ws_s[a][:, in_pass], v_w[h], v_s[h])
+                bank = product(ws_w[:, cols].bitcast(FP8X4), ws_s[:, cols], v_w[h], v_s[h])
                 nc.scalar.activation(out=x1[s][:, BANK * h : BANK * (h + 1)], in_=bank[:], func=ACT.Identity, bias=bs_cols[:, a, t : t + 1])
-            bank = product(w8_w[:, cols].bitcast(FP8X4), w8_s[:, cols], v2_w, v2_s)
+            bank = product(w8_w[:, cols].bitcast(FP8X4), w_s[:, H + P * s : H + P * (s + 1)], v2_w, v2_s)
             nc.scalar.copy(out=b[s][:], in_=bank[:])
-            for h in range(2):
-                bank = product(w4_w[:, 2 * P * s : 2 * P * (s + 1)].bitcast(FP4X4), w4_s[:, cols], v_w[h], v_s[h])
-                nc.scalar.copy(out=x2[s][:, BANK * h : BANK * (h + 1)], in_=bank[:])
+            scaled[s] = ring.tile([P, J], F32, name="scaled", bufs=3)
+            nc.vector.tensor_tensor(scaled[s][:], x1[s][:].indirect(pos_t[:]), b[s][:], ALU.mult)
 
-        def combine(s, j0, j1):
+        def shift_side(s, pieces):
             a, t = divmod(s, 4)
-            picks = pos_t[:, j0 // 16 : j1 // 16]
-            scaled = ring.tile([P, J], F32, name="scaled")
-            nc.vector.tensor_tensor(scaled[:, j0:j1], x1[s][:].indirect(picks), b[s][:, j0:j1], ALU.mult)
-            nc.vector.tensor_tensor(u[a][:, t, j0:j1], x2[s][:].indirect(picks), scaled[:, j0:j1], ALU.add)
+            for h in range(2):
+                bank = product(w4_w[:, 2 * P * s : 2 * P * (s + 1)].bitcast(FP4X4), w_s[:, P * s : P * (s + 1)], v_w[h], v_s[h])
+                nc.scalar.copy(out=x2[s][:, BANK * h : BANK * (h + 1)], in_=bank[:])
+            for j0, j1 in pieces:
+                nc.vector.tensor_tensor(u[a][:, t, j0:j1], x2[s][:].indirect(pos_t[:, j0 // 16 : j1 // 16]), scaled[s][:, j0:j1], ALU.add)
 
         def tanh(s, j0, j1):
             a, t = divmod(s, 4)
@@ -192,28 +184,27 @@ def tile_list_lint_autofix_edits_kernel(
             z_w = keep([P, width], U32, f"z_w{a}_{j0}")
             z_s = keep([P, width], U8, f"z_s{a}_{j0}")
             nc.vector.tensor_tensor(
-                z_b[:].rearrange("p (c i t) -> p c t i", t=4, i=4),
-                u[a][:, :, j0:j1].rearrange("p t (c i) -> p c t i", i=4),
-                late_cols[:, a, 0:4].unsqueeze(1).unsqueeze(3).to_broadcast([P, width // 4, 4, 4]),
+                z_b[:].rearrange("p (c i t) -> p c t i", t=4, i=2),
+                u[a][:, :, j0:j1].rearrange("p t (c i) -> p c t i", i=2),
+                late_cols[:, a, 0:4].unsqueeze(1).unsqueeze(3).to_broadcast([P, width // 2, 4, 2]),
                 ALU.mult,
             )
-            quantize(z_w, z_s, z_b)
+            quantize(z_w[:], z_s[:], z_b[:])
             return z_w, z_s
 
-        wo_b = [keep([P, 4 * N], BF16, f"wo_b{a}") for a in range(PASSES)]
-        wo_w = [keep([P, N], U32, f"wo_w{a}") for a in range(PASSES)]
-        wo_s = [keep([P, N], U8, f"wo_s{a}") for a in range(PASSES)]
+        wo_b = keep([P, PASSES * 4 * N], BF16, "wo_b")
+        wo_w = keep([P, PASSES * N], U32, "wo_w")
+        wo_s = keep([P, PASSES * N], U8, "wo_s")
 
-        def make_wo(a):
+        def round_wo(a):
             nc.vector.tensor_copy(
-                out=wo_b[a][:].rearrange("p (c i t) -> p c t i", t=4, i=4),
-                in_=wo_raw[a][:].rearrange("p t (c i) -> p c t i", i=4),
+                out=wo_b[:, 4 * N * a : 4 * N * (a + 1)].rearrange("p (c i t) -> p c t i", t=4, i=2),
+                in_=wo_raw[a][:].rearrange("p t (c i) -> p c t i", i=2),
             )
-            quantize(wo_w[a], wo_s[a], wo_b[a])
 
         def second_pass(acc, a, nt, words, plane):
-            cols = slice(P * nt, P * (nt + 1))
-            nc.tensor.matmul_mx(out=acc, lhsT=wo_w[a][:, cols].bitcast(FP8X4), lhsT_scale=wo_s[a][:, cols], rhs=words.bitcast(FP8X4), rhs_scale=plane, start=(a == 0), stop=(a == PASSES - 1))
+            cols = slice(N * a + P * nt, N * a + P * (nt + 1))
+            nc.tensor.matmul_mx(out=acc, lhsT=wo_w[:, cols].bitcast(FP8X4), lhsT_scale=wo_s[:, cols], rhs=words.bitcast(FP8X4), rhs_scale=plane, start=(a == 0), stop=(a == PASSES - 1))
 
         out_rows = out.rearrange("(b p) j -> p b j", p=P)
 
@@ -225,16 +216,15 @@ def tile_list_lint_autofix_edits_kernel(
 
         z0 = None
         late_cols = None
+        scale_side(0)
         for s in range(SLICES):
-            first_stage(s)
-            if s == 1:
-                round_ws(2)
-                round_ws(3)
-                quantize(ws_w[1], ws_s[1], ws_b[1])
-            if s < SLICES - 1:
-                combine(s, 0, J)
-            if s == 2 or s == 3:
-                make_wo(s - 2)
+            if s + 1 < SLICES:
+                scale_side(s + 1)
+            shift_side(s, [(0, J)] if s + 1 < SLICES else TAIL)
+            if s == 2:
+                round_wo(0)
+                round_wo(1)
+                quantize(wo_w[:], wo_s[:], wo_b[:])
             if s == 4:
                 late_cols = onto_partitions(rows[1], "late_cols")
             if s >= 2:
@@ -248,9 +238,7 @@ def tile_list_lint_autofix_edits_kernel(
         for nt in range(4):
             second_pass(last[nt][:, 0 : b1 - b0], 0, nt, z0[0][:, b0:b1], z0[1][:, b0:b1])
 
-        combine(SLICES - 1, a0, a1)
         tanh(SLICES - 1, a0, a1)
-        combine(SLICES - 1, b0, b1)
         tanh(SLICES - 1, b0, b1)
         z1 = make_z(1, a0, a1)
         z2 = make_z(1, b0, b1)

@@ -21,7 +21,7 @@ P = 128
 BANK = 512
 SLICES = H // P
 PASSES = H // 512
-TAIL = [(0, 256), (256, 512)]
+TAIL = [(0, 256), (256, 384), (384, 512)]
 
 
 def tile_list_lint_autofix_edits_kernel(
@@ -31,14 +31,17 @@ def tile_list_lint_autofix_edits_kernel(
     nc = tc.nc
     with ExitStack() as ctx:
         held = ctx.enter_context(tc.tile_pool(name="held", bufs=1))
-        ring = ctx.enter_context(tc.tile_pool(name="ring", bufs=2))
-        psum = ctx.enter_context(tc.psum_pool(name="psum", bufs=4))
+        ring = ctx.enter_context(tc.tile_pool(name="ring", bufs=4))
+        psum = ctx.enter_context(tc.psum_pool(name="psum", bufs=1))
 
-        def keep(shape, dtype, name):
-            return held.tile(shape, dtype, name=name, align_bytes=64)
+        def keep(shape, dtype, name, tag=""):
+            return held.tile(shape, dtype, name=name, tag=tag, align_bytes=64)
 
-        def load_plane(queue, plane, rows):
-            for q in range(4):
+        def work_bank(tag="scale"):
+            return psum.tile([P, BANK], F32, name="work", tag=tag, bufs=2 if tag == "proj" else 3)
+
+        def load_plane(queue, plane, rows, quadrants=range(4)):
+            for q in quadrants:
                 queue.dma_start(out=plane[32 * q : 32 * q + 4].bitcast(I32), in_=rows[0, 4 * q : 4 * q + 4, :].bitcast(I32))
 
         offs_t = held.tile([P, S // 16], U16, name="offs_t")
@@ -46,54 +49,57 @@ def tile_list_lint_autofix_edits_kernel(
         offs2_t = held.tile([P, J // 16], U16, name="offs2_t")
         tab_w = keep([P, T], U32, "tab_w")
         tab_s = keep([P, T], U8, "tab_s")
+        tab2_w = keep([P, T2], U32, "tab2_w")
         tab2_s = keep([P, T2], U8, "tab2_s")
-        w_s_raw = keep([P, 2 * H], U8, "w_s_raw")
-
-        nc.vector.memset(tab_s[:].bitcast(I32), 0)
-        nc.vector.memset(tab2_s[:].bitcast(I32), 0)
-        nc.vector.memset(w_s_raw[:].bitcast(I32), 0)
+        w8_s_raw = keep([P, H], U8, "w8_s_raw", tag="w8_s_raw")
+        w4_s_raw = keep([P, H], U8, "w4_s_raw", tag="w4_s_raw")
         rows = [keep([P, 2 * P], F32, f"rows{e}") for e in range(2)]
         ident = keep([P, P], F32, "ident")
+
+        nc.gpsimd.memset(tab_s[:].bitcast(I32), 0)
+        nc.vector.memset(w4_s_raw[:].bitcast(I32), 0)
+        nc.vector.memset(tab2_s[:].bitcast(I32), 0)
         nc.vector.memset(rows[0][:], 0.0)
+        nc.gpsimd.memset(w8_s_raw[:].bitcast(I32), 0)
+        nc.gpsimd.memset(rows[1][:], 0.0)
         make_identity(nc, ident[:])
-        load_plane(nc.gpsimd, tab2_s[:], tab2_scales)
-        with tc.tile_pool(name="first", bufs=1) as first:
-            warm = first.tile([P, 8], F32, name="warm")
-            nc.vector.memset(warm[:], 0.0)
-            nc.scalar.activation(out=warm[:, 0:1], in_=warm[:, 1:2], func=ACT.Tanh)
-        later = ctx.enter_context(tc.tile_pool(name="later", bufs=1))
 
         ws_rows = ws.rearrange("(p j) r -> p j r", j=4)
-        ws_raw = [keep([P, 4, 512], F32, "ws_raw0"), later.tile([P, 4, 512], F32, name="ws_raw1")]
-        wo_raw = [later.tile([P, 4, N], F32, name=f"wo_raw{a}") for a in range(PASSES)]
-        tab2_w = later.tile([P, T2], U32, name="tab2_w")
-        w8_w_raw = later.tile([P, H], I32, name="w8_w_raw")
-        w4_w_raw = later.tile([P, 2 * H], U8, name="w4_w_raw")
+        ws_raw = [keep([P, 4, 512], F32, f"ws_raw{a}") for a in range(PASSES)]
+        wo_raw = [keep([P, 4, N], F32, f"wo_raw{a}") for a in range(PASSES)]
+        w8_w_raw = [keep([P, 512], I32, f"w8_w_raw{a}") for a in range(PASSES)]
+        w4_w_raw = keep([P, 2 * H], U8, "w4_w_raw")
+        w8_rows = w8_words[0].rearrange("p c i -> p (c i)").bitcast(I32)
 
         by_slot = "(g t i) -> t g i"
         nc.sync.dma_start(offs_t[:], offs)
         nc.sync.dma_start(offs2_t[:], offs2)
-        nc.sync.dma_start(pos_t[:], pos1)
-        nc.sync.dma_start(out=tab_w[:].bitcast(I32), in_=tab_words[0].rearrange("p t i -> p (t i)").bitcast(I32))
-        nc.sync.dma_start(out=ws_raw[0][:], in_=ws_rows[:, :, 0:512])
         load_plane(nc.sync, tab_s[:], tab_scales)
-        nc.sync.dma_start(out=ws_raw[1][:], in_=ws_rows[:, :, 512:1024])
-        nc.sync.dma_start(out=rows[0][0:4, :].rearrange("t (g i) -> t g i", i=8), in_=bs.rearrange(by_slot, t=4, i=8))
-        load_plane(nc.sync, w_s_raw[:, H : 2 * H], w8_scales)
-        nc.sync.dma_start(out=tab2_w[:].bitcast(I32), in_=tab2_words[0].rearrange("p t i -> p (t i)").bitcast(I32))
-        nc.sync.dma_start(out=w8_w_raw[:], in_=w8_words[0].rearrange("p c i -> p (c i)").bitcast(I32))
-        load_plane(nc.sync, w_s_raw[:, 0:H], w4_scales)
+        nc.sync.dma_start(out=tab_w[:].bitcast(I32), in_=tab_words[0].rearrange("p t i -> p (t i)").bitcast(I32))
         nc.sync.dma_start(out=w4_w_raw[:].bitcast(I32), in_=w4_words[0].bitcast(I32))
+        load_plane(nc.sync, w4_s_raw[:], w4_scales)
+        nc.sync.dma_start(out=rows[0][0:4, :].rearrange("t (g i) -> t g i", i=8), in_=bs.rearrange(by_slot, t=4, i=8))
+        nc.sync.dma_start(out=ws_raw[0][:], in_=ws_rows[:, :, 0:512])
+        load_plane(nc.sync, tab2_s[:], tab2_scales)
+        nc.sync.dma_start(out=tab2_w[:].bitcast(I32), in_=tab2_words[0].rearrange("p t i -> p (t i)").bitcast(I32))
+        nc.sync.dma_start(out=w8_w_raw[0][:], in_=w8_rows[:, 0:512])
+        load_plane(nc.sync, w8_s_raw[:], w8_scales)
+        nc.sync.dma_start(pos_t[:], pos1)
         wo_rows = wo.rearrange("(a q t i) n -> a t q i n", a=PASSES, t=4, i=8)
-        for a in range(PASSES):
+
+        def load_wo(a):
             for t in range(4):
                 nc.sync.dma_start(out=wo_raw[a][:, t, :], in_=wo_rows[a, t])
-        nc.vector.memset(rows[1][:], 0.0)
+
+        nc.sync.dma_start(out=ws_raw[1][:], in_=ws_rows[:, :, 512:1024])
+        nc.sync.dma_start(out=w8_w_raw[1][:], in_=w8_rows[:, 512:1024])
+        load_wo(0)
         nc.sync.dma_start(out=rows[1][0:4, :].rearrange("t (g i) -> t g i", i=8), in_=gain.rearrange(by_slot, t=4, i=8))
         nc.sync.dma_start(out=rows[1][4:8, 0:P], in_=bo.rearrange("(b p) -> b p", p=P))
+        load_wo(1)
 
         def onto_partitions(staged, name):
-            turned = psum.tile([P, BANK], F32, name="work")
+            turned = work_bank("proj")
             for a in range(PASSES):
                 nc.tensor.transpose(turned[:, P * a : P * (a + 1)], staged[:, P * a : P * (a + 1)], ident[:])
             cols = keep([P, PASSES, 8], F32, name)
@@ -102,16 +108,17 @@ def tile_list_lint_autofix_edits_kernel(
 
         bs_cols = onto_partitions(rows[0], "bs_cols")
 
-        v_w = [keep([P, BANK], U32, f"v_w{h}") for h in range(2)]
-        v_s = [keep([P, BANK], U8, f"v_s{h}") for h in range(2)]
+        v_w = [keep([P, BANK], U32, "v_w0")]
+        w4_s = keep([P, H], U8, "w4_s")
+        v_s = keep([P, S], U8, "v_s")
         v2_w = keep([P, J], U32, "v2_w")
         v2_s = keep([P, J], U8, "v2_s")
         w4_w = keep([P, 2 * H], U8, "w4_w")
-        w_s = keep([P, 2 * H], U8, "w_s")
-        w8_w = keep([P, H], I32, "w8_w")
-        ws_b = [keep([P, 4 * 512], BF16, f"ws_b{a}") for a in range(PASSES)]
-        ws_w = keep([P, H], U32, "ws_w")
-        ws_s = keep([P, H], U8, "ws_s")
+        w8_s = keep([P, H], U8, "w8_s")
+        w8_first = keep([P, P], I32, "w8_first")
+        w8_w = [keep([P, 512], I32, f"w8_w{a}") for a in range(PASSES)]
+        ws_b = {0: keep([P, 4 * 512], BF16, "ws_b0")}
+        ws_q = {}
 
         def reorder(dst, src, groups):
             nc.vector.tensor_copy(
@@ -119,9 +126,9 @@ def tile_list_lint_autofix_edits_kernel(
                 in_=src.rearrange("p (a q t i) -> p a q t i", a=groups, t=4, q=16),
             )
 
-        def round_ws(s):
+        def round_ws(s, copy):
             a, t = divmod(s, 4)
-            nc.scalar.copy(
+            copy(
                 out=ws_b[a][:, 512 * t : 512 * (t + 1)].rearrange("p (q i e j) -> p q i j e", q=16, e=2, j=4),
                 in_=ws_raw[a][:].rearrange("p j (q t i e) -> p t q i j e", t=4, i=4, e=2)[:, t],
             )
@@ -129,48 +136,71 @@ def tile_list_lint_autofix_edits_kernel(
         def quantize(words, plane, src):
             nc.vector.quantize_mx(out=words.bitcast(FP8X4), scales=plane, in_=src)
 
-        for s in range(SLICES):
-            round_ws(s)
-        for h in range(2):
-            nc.vector.tensor_copy(out=v_w[h][:], in_=tab_w[:].indirect(offs_t[:, 32 * h : 32 * (h + 1)]))
-        for h in range(2):
-            nc.vector.tensor_copy(out=v_s[h][:], in_=tab_s[:].indirect(offs_t[:, 32 * h : 32 * (h + 1)]))
-        for half in range(2):
-            quantize(ws_w[:, 256 * half : 256 * (half + 1)], ws_s[:, 256 * half : 256 * (half + 1)], ws_b[0][:, 1024 * half : 1024 * (half + 1)])
+        def quantize_ws(s0, s1, tag=""):
+            a, t = divmod(s0, 4)
+            words = keep([P, P * (s1 - s0)], U32, f"ws_w{s0}", tag=tag)
+            plane = keep([P, P * (s1 - s0)], U8, f"ws_s{s0}")
+            quantize(words[:], plane[:], ws_b[a][:, 512 * t : 512 * (t + s1 - s0)])
+            for s in range(s0, s1):
+                cols = slice(P * (s - s0), P * (s - s0 + 1))
+                ws_q.update({s: (words[:, cols], plane[:, cols])})
+
+        nc.vector.tensor_copy(out=v_s[:], in_=tab_s[:].indirect(offs_t[:]))
+        nc.vector.tensor_copy(out=v_w[0][:], in_=tab_w[:].indirect(offs_t[:, 0:32]))
+        reorder(w4_w[:].bitcast(I32), w4_w_raw[:].bitcast(I32), PASSES)
+        reorder(w4_s[:].bitcast(I32), w4_s_raw[:].bitcast(I32), PASSES)
+        v_w.append(keep([P, BANK], U32, "v_w1", tag="w4_s_raw"))
+        nc.vector.tensor_copy(out=v_w[1][:], in_=tab_w[:].indirect(offs_t[:, 32:64]))
+        for s in range(4):
+            round_ws(s, nc.vector.tensor_copy)
+        quantize_ws(0, 2)
         nc.vector.tensor_copy(out=v2_s[:], in_=tab2_s[:].indirect(offs2_t[:]))
         nc.vector.tensor_copy(out=v2_w[:], in_=tab2_w[:].indirect(offs2_t[:]))
-        reorder(w8_w[:], w8_w_raw[:], PASSES)
-        reorder(w_s[:].bitcast(I32), w_s_raw[:].bitcast(I32), 2 * PASSES)
-        reorder(w4_w[:].bitcast(I32), w4_w_raw[:].bitcast(I32), PASSES)
-        quantize(ws_w[:, 512:1024], ws_s[:, 512:1024], ws_b[1][:])
+        reorder(w8_s[:].bitcast(I32), w8_s_raw[:].bitcast(I32), PASSES)
+        by_slice = w8_w_raw[0][:].rearrange("p (q t i) -> p t q i", t=4, q=16)
+        nc.vector.tensor_copy(out=w8_first[:].rearrange("p (q i) -> p q i", q=16), in_=by_slice[:, 0])
+        nc.vector.tensor_copy(
+            out=w8_w[0][:, P:512].rearrange("p (t q i) -> p q t i", t=3, q=16),
+            in_=w8_w_raw[0][:].rearrange("p (q t i) -> p q t i", t=4, q=16)[:, :, 1:4, :],
+        )
+        quantize_ws(2, 4, tag="w8_s_raw")
 
-        x1 = [keep([P, S], F32, f"x1_{s}") for s in range(SLICES)]
-        x2 = [keep([P, S], F32, f"x2_{s}") for s in range(SLICES)]
-        b = [keep([P, J], F32, f"b_{s}") for s in range(SLICES)]
+        x1 = {}
+        x2 = {}
+        b = [keep([P, J], F32, f"b_{s}", tag=f"b_{s}") for s in range(SLICES)]
         scaled = {}
         u = [keep([P, 4, J], F32, f"u_{a}") for a in range(PASSES)]
 
-        def product(lhsT, lhsT_scale, words, plane):
-            bank = psum.tile([P, BANK], F32, name="work")
-            nc.tensor.matmul_mx(out=bank[:], lhsT=lhsT, lhsT_scale=lhsT_scale, rhs=words[:].bitcast(FP8X4), rhs_scale=plane[:], start=True, stop=True)
+        def product(lhsT, lhsT_scale, words, plane, tag="scale"):
+            bank = work_bank(tag)
+            nc.tensor.matmul_mx(out=bank[:], lhsT=lhsT, lhsT_scale=lhsT_scale, rhs=words.bitcast(FP8X4), rhs_scale=plane, start=True, stop=True)
             return bank
+
+        def make_x1(s, halves=range(2)):
+            a, t = divmod(s, 4)
+            if s not in x1:
+                x1.update({s: keep([P, S], F32, f"x1_{s}", tag=f"x1_{s}")})
+            for h in halves:
+                bank = product(ws_q[s][0].bitcast(FP8X4), ws_q[s][1], v_w[h][:], v_s[:, BANK * h : BANK * (h + 1)])
+                nc.scalar.activation(out=x1[s][:, BANK * h : BANK * (h + 1)], in_=bank[:], func=ACT.Identity, bias=bs_cols[:, a, t : t + 1])
 
         def scale_side(s):
             a, t = divmod(s, 4)
-            cols = slice(P * s, P * (s + 1))
-            for h in range(2):
-                bank = product(ws_w[:, cols].bitcast(FP8X4), ws_s[:, cols], v_w[h], v_s[h])
-                nc.scalar.activation(out=x1[s][:, BANK * h : BANK * (h + 1)], in_=bank[:], func=ACT.Identity, bias=bs_cols[:, a, t : t + 1])
-            bank = product(w8_w[:, cols].bitcast(FP8X4), w_s[:, H + P * s : H + P * (s + 1)], v2_w, v2_s)
+            words = w8_first[:] if s == 0 else w8_w[a][:, P * t : P * (t + 1)]
+            bank = product(words.bitcast(FP8X4), w8_s[:, P * s : P * (s + 1)], v2_w[:], v2_s[:], "proj")
             nc.scalar.copy(out=b[s][:], in_=bank[:])
-            scaled[s] = ring.tile([P, J], F32, name="scaled", bufs=3)
+            scaled[s] = ring.tile([P, J], F32, name="scaled")
             nc.vector.tensor_tensor(scaled[s][:], x1[s][:].indirect(pos_t[:]), b[s][:], ALU.mult)
+
+        def make_x2(s, halves=range(2)):
+            if s not in x2:
+                x2.update({s: keep([P, S], F32, f"x2_{s}", tag=f"x2_{s}" if s < 3 else f"x1_{s - 3}")})
+            for h in halves:
+                bank = product(w4_w[:, 2 * P * s : 2 * P * (s + 1)].bitcast(FP4X4), w4_s[:, P * s : P * (s + 1)], v_w[h][:], v_s[:, BANK * h : BANK * (h + 1)], "shift")
+                nc.scalar.copy(out=x2[s][:, BANK * h : BANK * (h + 1)], in_=bank[:])
 
         def shift_side(s, pieces):
             a, t = divmod(s, 4)
-            for h in range(2):
-                bank = product(w4_w[:, 2 * P * s : 2 * P * (s + 1)].bitcast(FP4X4), w_s[:, P * s : P * (s + 1)], v_w[h], v_s[h])
-                nc.scalar.copy(out=x2[s][:, BANK * h : BANK * (h + 1)], in_=bank[:])
             for j0, j1 in pieces:
                 nc.vector.tensor_tensor(u[a][:, t, j0:j1], x2[s][:].indirect(pos_t[:, j0 // 16 : j1 // 16]), scaled[s][:, j0:j1], ALU.add)
 
@@ -178,86 +208,141 @@ def tile_list_lint_autofix_edits_kernel(
             a, t = divmod(s, 4)
             nc.scalar.activation(out=u[a][:, t, j0:j1], in_=u[a][:, t, j0:j1], func=ACT.Tanh)
 
-        def make_z(a, j0, j1):
+        def apply_gain(a, j0, j1):
             width = j1 - j0
             z_b = keep([P, 4 * width], BF16, f"z_b{a}_{j0}")
-            z_w = keep([P, width], U32, f"z_w{a}_{j0}")
-            z_s = keep([P, width], U8, f"z_s{a}_{j0}")
             nc.vector.tensor_tensor(
                 z_b[:].rearrange("p (c i t) -> p c t i", t=4, i=2),
                 u[a][:, :, j0:j1].rearrange("p t (c i) -> p c t i", i=2),
                 late_cols[:, a, 0:4].unsqueeze(1).unsqueeze(3).to_broadcast([P, width // 2, 4, 2]),
                 ALU.mult,
             )
+            return z_b
+
+        def quantize_z(z_b, name):
+            width = z_b.shape[1] // 4
+            z_w = keep([P, width], U32, f"z_w{name}")
+            z_s = keep([P, width], U8, f"z_s{name}")
             quantize(z_w[:], z_s[:], z_b[:])
             return z_w, z_s
 
-        wo_b = keep([P, PASSES * 4 * N], BF16, "wo_b")
+        wo_b = [keep([P, 4 * N], BF16, f"wo_b{a}") for a in range(PASSES)]
         wo_w = keep([P, PASSES * N], U32, "wo_w")
         wo_s = keep([P, PASSES * N], U8, "wo_s")
 
-        def round_wo(a):
-            nc.vector.tensor_copy(
-                out=wo_b[:, 4 * N * a : 4 * N * (a + 1)].rearrange("p (c i t) -> p c t i", t=4, i=2),
+        def round_wo(a, copy):
+            copy(
+                out=wo_b[a][:].rearrange("p (c i t) -> p c t i", t=4, i=2),
                 in_=wo_raw[a][:].rearrange("p t (c i) -> p c t i", i=2),
             )
 
-        def second_pass(acc, a, nt, words, plane):
+        def quantize_wo(a):
+            quantize(wo_w[:, N * a : N * (a + 1)], wo_s[:, N * a : N * (a + 1)], wo_b[a][:])
+
+        def second_pass(acc, a, nt, words, plane, start, stop):
             cols = slice(N * a + P * nt, N * a + P * (nt + 1))
-            nc.tensor.matmul_mx(out=acc, lhsT=wo_w[:, cols].bitcast(FP8X4), lhsT_scale=wo_s[:, cols], rhs=words.bitcast(FP8X4), rhs_scale=plane, start=(a == 0), stop=(a == PASSES - 1))
+            nc.tensor.matmul_mx(out=acc, lhsT=wo_w[:, cols].bitcast(FP8X4), lhsT_scale=wo_s[:, cols], rhs=words.bitcast(FP8X4), rhs_scale=plane, start=start, stop=stop)
 
         out_rows = out.rearrange("(b p) j -> p b j", p=P)
 
-        def finish(acc, res, nt, on_scalar):
-            if on_scalar:
-                nc.scalar.activation(out=res, in_=acc, func=ACT.Identity, bias=late_cols[:, 0, 4 + nt : 5 + nt])
-            else:
-                nc.vector.tensor_scalar(res, acc, late_cols[:, 0, 4 + nt : 5 + nt], None, ALU.add)
-
-        z0 = None
-        late_cols = None
+        for h in range(2):
+            for s in range(3):
+                make_x2(s, [h])
+        make_x1(0)
+        make_x1(1)
         scale_side(0)
-        for s in range(SLICES):
+        scale_side(1)
+        shift_side(0, [(0, J)])
+        make_x1(2)
+        scale_side(2)
+        ws_b.update({1: keep([P, 4 * 512], BF16, "ws_b1", tag="b_0")})
+        for s in range(4, SLICES):
+            round_ws(s, nc.scalar.copy)
+        shift_side(1, [(0, J)])
+        quantize_ws(4, 8)
+        reorder(w8_w[1][:], w8_w_raw[1][:], 1)
+        make_x1(3)
+        scale_side(3)
+        make_x2(3)
+        shift_side(2, [(0, J)])
+        round_wo(0, nc.vector.tensor_copy)
+        shift_side(3, [(0, J)])
+        quantize_wo(0)
+        make_x1(4)
+        scale_side(4)
+        make_x2(4)
+        late_cols = onto_partitions(rows[1], "late_cols")
+        for s in range(4):
+            tanh(s, 0, J)
+        for s in range(4, SLICES):
             if s + 1 < SLICES:
+                make_x1(s + 1)
                 scale_side(s + 1)
-            shift_side(s, [(0, J)] if s + 1 < SLICES else TAIL)
-            if s == 2:
-                round_wo(0)
-                round_wo(1)
-                quantize(wo_w[:], wo_s[:], wo_b[:])
             if s == 4:
-                late_cols = onto_partitions(rows[1], "late_cols")
-            if s >= 2:
-                tanh(s - 2, 0, J)
+                z0_b = apply_gain(0, 0, J)
             if s == 5:
-                z0 = make_z(0, 0, J)
-        tanh(SLICES - 2, 0, J)
+                round_wo(1, nc.scalar.copy)
+            if s > 4:
+                make_x2(s)
+            shift_side(s, [(0, J)] if s + 1 < SLICES else TAIL)
+            if s == 4:
+                z0 = quantize_z(z0_b, "0")
+            if s == 5:
+                quantize_wo(1)
+        for s in range(4, SLICES - 1):
+            tanh(s, 0, J)
 
-        (a0, a1), (b0, b1) = TAIL
-        last = [psum.tile([P, BANK], F32, name="last") for nt in range(4)]
+        (a0, a1), (b0, b1), (c0, c1) = TAIL
+        bank_b = work_bank("proj")
+        bank_c = [work_bank("shift") for pair in range(2)]
         for nt in range(4):
-            second_pass(last[nt][:, 0 : b1 - b0], 0, nt, z0[0][:, b0:b1], z0[1][:, b0:b1])
+            second_pass(bank_b[:, P * nt : P * (nt + 1)], 0, nt, z0[0][:, b0:b1], z0[1][:, b0:b1], nt == 0, False)
+        for nt in range(4):
+            pair, e = divmod(nt, 2)
+            second_pass(bank_c[pair][:, P * e : P * (e + 1)], 0, nt, z0[0][:, c0:c1], z0[1][:, c0:c1], e == 0, False)
 
-        tanh(SLICES - 1, a0, a1)
-        tanh(SLICES - 1, b0, b1)
-        z1 = make_z(1, a0, a1)
-        z2 = make_z(1, b0, b1)
+        for j0, j1 in TAIL:
+            tanh(SLICES - 1, j0, j1)
+        za_b = apply_gain(1, a0, a1)
+        zb_b = apply_gain(1, b0, b1)
+        za = quantize_z(za_b, "a")
+        zc_b = apply_gain(1, c0, c1)
+        zb = quantize_z(zb_b, "b")
+        zc = quantize_z(zc_b, "c")
+
+        def add_bias(res, acc, nt):
+            nc.scalar.activation(out=res, in_=acc, func=ACT.Identity, bias=late_cols[:, 0, 4 + nt : 5 + nt])
+
         for pair in range(2):
-            bank = psum.tile([P, BANK], F32, name="work")
+            bank = work_bank()
             res = keep([P, 2, a1 - a0], F32, f"res_a{pair}")
             for e in range(2):
                 nt = 2 * pair + e
-                acc = bank[:, 256 * e : 256 * e + a1 - a0]
-                second_pass(acc, 0, nt, z0[0][:, a0:a1], z0[1][:, a0:a1])
-                second_pass(acc, 1, nt, z1[0][:], z1[1][:])
+                acc = bank[:, 256 * e : 256 * (e + 1)]
+                second_pass(acc, 0, nt, z0[0][:, a0:a1], z0[1][:, a0:a1], True, False)
+                second_pass(acc, 1, nt, za[0][:], za[1][:], False, True)
             for e in range(2):
-                finish(bank[:, 256 * e : 256 * e + a1 - a0], res[:, e, :], 2 * pair + e, True)
+                add_bias(res[:, e, :], bank[:, 256 * e : 256 * (e + 1)], 2 * pair + e)
             nc.sync.dma_start(out=out_rows[:, 2 * pair : 2 * pair + 2, a0:a1], in_=res[:])
+
         for nt in range(4):
-            second_pass(last[nt][:, 0 : b1 - b0], 1, nt, z2[0][:], z2[1][:])
-        for pair in range(2):
-            res = keep([P, 2, b1 - b0], F32, f"res_b{pair}")
-            for e in range(2):
-                nt = 2 * pair + e
-                finish(last[nt][:, 0 : b1 - b0], res[:, e, :], nt, e == 0)
-            nc.sync.dma_start(out=out_rows[:, 2 * pair : 2 * pair + 2, b0:b1], in_=res[:])
+            second_pass(bank_b[:, P * nt : P * (nt + 1)], 1, nt, zb[0][:], zb[1][:], False, nt == 3)
+        res_b = keep([P, 4, b1 - b0], F32, "res_b")
+        for nt in range(4):
+            add_bias(res_b[:, nt, :], bank_b[:, P * nt : P * (nt + 1)], nt)
+        nc.sync.dma_start(out=out_rows[:, :, b0:b1], in_=res_b[:])
+
+        for nt in range(4):
+            pair, e = divmod(nt, 2)
+            second_pass(bank_c[pair][:, P * e : P * (e + 1)], 1, nt, zc[0][:], zc[1][:], False, e == 1)
+        res_c = [keep([P, 2, c1 - c0], F32, f"res_c{pair}") for pair in range(2)]
+        for e in range(2):
+            add_bias(res_c[0][:, e, :], bank_c[0][:, P * e : P * (e + 1)], e)
+        nc.scalar.dma_start(out=out_rows[:, 0:2, c0:c1], in_=res_c[0][:])
+        nc.vector.tensor_tensor(
+            res_c[1][:],
+            bank_c[1][:, 0 : 2 * P].rearrange("p (e j) -> p e j", e=2),
+            late_cols[:, 0, 6:8].unsqueeze(2).to_broadcast([P, 2, c1 - c0]),
+            ALU.add,
+        )
+        nc.sync.dma_start(out=out_rows[:, 2:4, c0:c1], in_=res_c[1][:])

@@ -129,8 +129,8 @@ def tile_list_lint_autofix_edits_kernel(
         def round_ws(s, copy):
             a, t = divmod(s, 4)
             copy(
-                out=ws_b[a][:, 512 * t : 512 * (t + 1)].rearrange("p (q i e j) -> p q i j e", q=16, e=2, j=4),
-                in_=ws_raw[a][:].rearrange("p j (q t i e) -> p t q i j e", t=4, i=4, e=2)[:, t],
+                out=ws_b[a][:, 512 * t : 512 * (t + 1)].rearrange("p (q i e j) -> p q i j e", q=16, e=4, j=4),
+                in_=ws_raw[a][:].rearrange("p j (q t i e) -> p t q i j e", t=4, i=2, e=4)[:, t],
             )
 
         def quantize(words, plane, src):
@@ -212,9 +212,9 @@ def tile_list_lint_autofix_edits_kernel(
             width = j1 - j0
             z_b = keep([P, 4 * width], BF16, f"z_b{a}_{j0}")
             nc.vector.tensor_tensor(
-                z_b[:].rearrange("p (c i t) -> p c t i", t=4, i=2),
-                u[a][:, :, j0:j1].rearrange("p t (c i) -> p c t i", i=2),
-                late_cols[:, a, 0:4].unsqueeze(1).unsqueeze(3).to_broadcast([P, width // 2, 4, 2]),
+                z_b[:].rearrange("p (c i t) -> p c t i", t=4, i=4),
+                u[a][:, :, j0:j1].rearrange("p t (c i) -> p c t i", i=4),
+                late_cols[:, a, 0:4].unsqueeze(1).unsqueeze(3).to_broadcast([P, width // 4, 4, 4]),
                 ALU.mult,
             )
             return z_b
@@ -232,8 +232,8 @@ def tile_list_lint_autofix_edits_kernel(
 
         def round_wo(a, copy):
             copy(
-                out=wo_b[a][:].rearrange("p (c i t) -> p c t i", t=4, i=2),
-                in_=wo_raw[a][:].rearrange("p t (c i) -> p c t i", i=2),
+                out=wo_b[a][:].rearrange("p (c i t) -> p c t i", t=4, i=4),
+                in_=wo_raw[a][:].rearrange("p t (c i) -> p c t i", i=4),
             )
 
         def quantize_wo(a):

@@ -21,7 +21,8 @@ P = 128
 BANK = 512
 SLICES = H // P
 PASSES = H // 512
-TAIL = [(0, 256), (256, 384), (384, 512)]
+TAIL = [(j0, j0 + P) for j0 in range(0, J, P)]
+WHOLE = 2
 
 
 def tile_list_lint_autofix_edits_kernel(
@@ -219,9 +220,9 @@ def tile_list_lint_autofix_edits_kernel(
             )
             return z_b
 
-        def quantize_z(z_b, name):
+        def quantize_z(z_b, name, tag=""):
             width = z_b.shape[1] // 4
-            z_w = keep([P, width], U32, f"z_w{name}")
+            z_w = keep([P, width], U32, f"z_w{name}", tag=tag)
             z_s = keep([P, width], U8, f"z_s{name}")
             quantize(z_w[:], z_s[:], z_b[:])
             return z_w, z_s
@@ -230,10 +231,10 @@ def tile_list_lint_autofix_edits_kernel(
         wo_w = keep([P, PASSES * N], U32, "wo_w")
         wo_s = keep([P, PASSES * N], U8, "wo_s")
 
-        def round_wo(a, copy):
+        def round_wo(a, copy, n0=0, n1=N):
             copy(
-                out=wo_b[a][:].rearrange("p (c i t) -> p c t i", t=4, i=4),
-                in_=wo_raw[a][:].rearrange("p t (c i) -> p c t i", i=4),
+                out=wo_b[a][:, 4 * n0 : 4 * n1].rearrange("p (c i t) -> p c t i", t=4, i=4),
+                in_=wo_raw[a][:, :, n0:n1].rearrange("p t (c i) -> p c t i", i=4),
             )
 
         def quantize_wo(a):
@@ -281,68 +282,57 @@ def tile_list_lint_autofix_edits_kernel(
             if s == 4:
                 z0_b = apply_gain(0, 0, J)
             if s == 5:
-                round_wo(1, nc.scalar.copy)
+                round_wo(1, nc.scalar.copy, 0, 256)
+                round_wo(1, nc.vector.tensor_copy, 256, N)
             if s > 4:
                 make_x2(s)
             shift_side(s, [(0, J)] if s + 1 < SLICES else TAIL)
-            if s == 4:
-                z0 = quantize_z(z0_b, "0")
             if s == 5:
                 quantize_wo(1)
         for s in range(4, SLICES - 1):
             tanh(s, 0, J)
 
-        (a0, a1), (b0, b1), (c0, c1) = TAIL
-        bank_b = work_bank("proj")
-        bank_c = [work_bank("shift") for pair in range(2)]
-        for nt in range(4):
-            second_pass(bank_b[:, P * nt : P * (nt + 1)], 0, nt, z0[0][:, b0:b1], z0[1][:, b0:b1], nt == 0, False)
-        for nt in range(4):
-            pair, e = divmod(nt, 2)
-            second_pass(bank_c[pair][:, P * e : P * (e + 1)], 0, nt, z0[0][:, c0:c1], z0[1][:, c0:c1], e == 0, False)
+        z0 = quantize_z(z0_b, "0", tag="x1_7")
 
+        banks = [[work_bank()] * 2 for piece in range(WHOLE)] + [[work_bank("shift"), work_bank(tag)] for tag in ("scale", "shift")]
+
+        def second_stage(a, piece, words, plane):
+            split = piece >= WHOLE
+            for nt in range(4):
+                first = nt % 2 == 0 if split else nt == 0
+                last = nt % 2 == 1 if split else nt == 3
+                second_pass(banks[piece][nt // 2][:, P * nt : P * (nt + 1)], a, nt, words, plane, a == 0 and first, a == 1 and last)
+
+        for piece, (j0, j1) in enumerate(TAIL):
+            second_stage(0, piece, z0[0][:, j0:j1], z0[1][:, j0:j1])
         for j0, j1 in TAIL:
             tanh(SLICES - 1, j0, j1)
-        za_b = apply_gain(1, a0, a1)
-        zb_b = apply_gain(1, b0, b1)
-        za = quantize_z(za_b, "a")
-        zc_b = apply_gain(1, c0, c1)
-        zb = quantize_z(zb_b, "b")
-        zc = quantize_z(zc_b, "c")
+        z_b = [apply_gain(1, *TAIL[0])]
+        z1 = []
+        for piece in range(len(TAIL)):
+            if piece + 1 < len(TAIL):
+                z_b.append(apply_gain(1, *TAIL[piece + 1]))
+            z1.append(quantize_z(z_b[piece], f"1_{piece}"))
 
         def add_bias(res, acc, nt):
             nc.scalar.activation(out=res, in_=acc, func=ACT.Identity, bias=late_cols[:, 0, 4 + nt : 5 + nt])
 
-        for pair in range(2):
-            bank = work_bank()
-            res = keep([P, 2, a1 - a0], F32, f"res_a{pair}")
-            for e in range(2):
-                nt = 2 * pair + e
-                acc = bank[:, 256 * e : 256 * (e + 1)]
-                second_pass(acc, 0, nt, z0[0][:, a0:a1], z0[1][:, a0:a1], True, False)
-                second_pass(acc, 1, nt, za[0][:], za[1][:], False, True)
-            for e in range(2):
-                add_bias(res[:, e, :], bank[:, 256 * e : 256 * (e + 1)], 2 * pair + e)
-            nc.sync.dma_start(out=out_rows[:, 2 * pair : 2 * pair + 2, a0:a1], in_=res[:])
-
-        for nt in range(4):
-            second_pass(bank_b[:, P * nt : P * (nt + 1)], 1, nt, zb[0][:], zb[1][:], False, nt == 3)
-        res_b = keep([P, 4, b1 - b0], F32, "res_b")
-        for nt in range(4):
-            add_bias(res_b[:, nt, :], bank_b[:, P * nt : P * (nt + 1)], nt)
-        nc.sync.dma_start(out=out_rows[:, :, b0:b1], in_=res_b[:])
-
-        for nt in range(4):
-            pair, e = divmod(nt, 2)
-            second_pass(bank_c[pair][:, P * e : P * (e + 1)], 1, nt, zc[0][:], zc[1][:], False, e == 1)
-        res_c = [keep([P, 2, c1 - c0], F32, f"res_c{pair}") for pair in range(2)]
-        for e in range(2):
-            add_bias(res_c[0][:, e, :], bank_c[0][:, P * e : P * (e + 1)], e)
-        nc.scalar.dma_start(out=out_rows[:, 0:2, c0:c1], in_=res_c[0][:])
-        nc.vector.tensor_tensor(
-            res_c[1][:],
-            bank_c[1][:, 0 : 2 * P].rearrange("p (e j) -> p e j", e=2),
-            late_cols[:, 0, 6:8].unsqueeze(2).to_broadcast([P, 2, c1 - c0]),
-            ALU.add,
-        )
-        nc.sync.dma_start(out=out_rows[:, 2:4, c0:c1], in_=res_c[1][:])
+        for piece, (j0, j1) in enumerate(TAIL):
+            second_stage(1, piece, z1[piece][0][:], z1[piece][1][:])
+            if piece < WHOLE:
+                res = keep([P, 4, P], F32, f"res{piece}")
+                for nt in range(4):
+                    add_bias(res[:, nt, :], banks[piece][0][:, P * nt : P * (nt + 1)], nt)
+                nc.sync.dma_start(out=out_rows[:, :, j0:j1], in_=res[:])
+            else:
+                res = [keep([P, 2, P], F32, f"res{piece}_{pair}") for pair in range(2)]
+                for nt in range(2):
+                    add_bias(res[0][:, nt, :], banks[piece][0][:, P * nt : P * (nt + 1)], nt)
+                nc.scalar.dma_start(out=out_rows[:, 0:2, j0:j1], in_=res[0][:])
+                nc.vector.tensor_tensor(
+                    res[1][:],
+                    banks[piece][1][:, 2 * P : 4 * P].rearrange("p (e j) -> p e j", e=2),
+                    late_cols[:, 0, 6:8].unsqueeze(2).to_broadcast([P, 2, P]),
+                    ALU.add,
+                )
+                nc.sync.dma_start(out=out_rows[:, 2:4, j0:j1], in_=res[1][:])

@@ -43,7 +43,7 @@ def tile_list_lint_autofix_edits_kernel(
 
         def load_plane(queue, plane, rows, quadrants=range(4)):
             for q in quadrants:
-                queue.dma_start(out=plane[32 * q : 32 * q + 4].bitcast(I32), in_=rows[0, 4 * q : 4 * q + 4, :].bitcast(I32))
+                queue.dma_start(out=plane[q:P:32].bitcast(I32), in_=rows[0, q:16:4, :].bitcast(I32))
 
         offs_t = held.tile([P, S // 16], U16, name="offs_t")
         pos_t = held.tile([P, J // 16], U16, name="pos_t")
@@ -74,10 +74,10 @@ def tile_list_lint_autofix_edits_kernel(
 
         by_slot = "(g t i) -> t g i"
         nc.sync.dma_start(offs_t[:], offs)
-        nc.sync.dma_start(offs2_t[:], offs2)
+        nc.sync.dma_start(out=w4_w_raw[:].bitcast(I32), in_=w4_words[0].bitcast(I32))
         load_plane(nc.sync, tab_s[:], tab_scales)
         nc.sync.dma_start(out=tab_w[:].bitcast(I32), in_=tab_words[0].rearrange("p t i -> p (t i)").bitcast(I32))
-        nc.sync.dma_start(out=w4_w_raw[:].bitcast(I32), in_=w4_words[0].bitcast(I32))
+        nc.sync.dma_start(offs2_t[:], offs2)
         load_plane(nc.sync, w4_s_raw[:], w4_scales)
         nc.sync.dma_start(out=rows[0][0:4, :].rearrange("t (g i) -> t g i", i=8), in_=bs.rearrange(by_slot, t=4, i=8))
         nc.sync.dma_start(out=ws_raw[0][:], in_=ws_rows[:, :, 0:512])
@@ -146,9 +146,9 @@ def tile_list_lint_autofix_edits_kernel(
                 cols = slice(P * (s - s0), P * (s - s0 + 1))
                 ws_q.update({s: (words[:, cols], plane[:, cols])})
 
+        reorder(w4_w[:].bitcast(I32), w4_w_raw[:].bitcast(I32), PASSES)
         nc.vector.tensor_copy(out=v_s[:], in_=tab_s[:].indirect(offs_t[:]))
         nc.vector.tensor_copy(out=v_w[0][:], in_=tab_w[:].indirect(offs_t[:, 0:32]))
-        reorder(w4_w[:].bitcast(I32), w4_w_raw[:].bitcast(I32), PASSES)
         reorder(w4_s[:].bitcast(I32), w4_s_raw[:].bitcast(I32), PASSES)
         v_w.append(keep([P, BANK], U32, "v_w1", tag="w4_s_raw"))
         nc.vector.tensor_copy(out=v_w[1][:], in_=tab_w[:].indirect(offs_t[:, 32:64]))

@@ -68,7 +68,7 @@ def tile_list_lint_autofix_edits_kernel(
         ws_rows = ws.rearrange("(p j) r -> p j r", j=4)
         ws_raw = [keep([P, 4, 512], F32, f"ws_raw{a}") for a in range(PASSES)]
         wo_raw = [keep([P, 4, N], F32, f"wo_raw{a}") for a in range(PASSES)]
-        w8_w_raw = [keep([P, 512], I32, f"w8_w_raw{a}") for a in range(PASSES)]
+        w8_w_raw = [keep([P, 512], I32, "w8_w_raw0")]
         w4_w_raw = keep([P, 2 * H], U8, "w4_w_raw")
         w8_rows = w8_words[0].rearrange("p c i -> p (c i)").bitcast(I32)
 
@@ -85,7 +85,6 @@ def tile_list_lint_autofix_edits_kernel(
         nc.sync.dma_start(out=tab2_w[:].bitcast(I32), in_=tab2_words[0].rearrange("p t i -> p (t i)").bitcast(I32))
         nc.sync.dma_start(out=w8_w_raw[0][:], in_=w8_rows[:, 0:512])
         load_plane(nc.sync, w8_s_raw[:], w8_scales)
-        nc.sync.dma_start(pos_t[:], pos1)
         wo_rows = wo.rearrange("(a q t i) n -> a t q i n", a=PASSES, t=4, i=8)
 
         def load_wo(a):
@@ -93,7 +92,13 @@ def tile_list_lint_autofix_edits_kernel(
                 nc.sync.dma_start(out=wo_raw[a][:, t, :], in_=wo_rows[a, t])
 
         nc.sync.dma_start(out=ws_raw[1][:], in_=ws_rows[:, :, 512:1024])
-        nc.sync.dma_start(out=w8_w_raw[1][:], in_=w8_rows[:, 512:1024])
+        nc.sync.dma_start(pos_t[:], pos1)
+        w8_late = keep([P, 512], I32, "w8_late")
+        for t in range(4):
+            nc.sync.dma_start(
+                out=w8_late[:, P * t : P * (t + 1)].rearrange("p (q i) -> p q i", i=8),
+                in_=w8_rows[:, 512:1024].rearrange("p (q t i) -> p t q i", t=4, i=8)[:, t],
+            )
         load_wo(0)
         nc.sync.dma_start(out=rows[1][0:4, :].rearrange("t (g i) -> t g i", i=8), in_=gain.rearrange(by_slot, t=4, i=8))
         nc.sync.dma_start(out=rows[1][4:8, 0:P], in_=bo.rearrange("(b p) -> b p", p=P))
@@ -117,8 +122,8 @@ def tile_list_lint_autofix_edits_kernel(
         w4_w = keep([P, 2 * H], U8, "w4_w")
         w8_s = keep([P, H], U8, "w8_s")
         w8_first = keep([P, P], I32, "w8_first")
-        w8_w = [keep([P, 512], I32, f"w8_w{a}") for a in range(PASSES)]
-        ws_b = {0: keep([P, 4 * 512], BF16, "ws_b0")}
+        w8_w = [keep([P, 512], I32, "w8_w0"), w8_late]
+        ws_b = {}
         ws_q = {}
 
         def reorder(dst, src, groups):
@@ -127,10 +132,12 @@ def tile_list_lint_autofix_edits_kernel(
                 in_=src.rearrange("p (a q t i) -> p a q t i", a=groups, t=4, q=16),
             )
 
-        def round_ws(s, copy):
+        def round_ws(s, copy, tag=""):
             a, t = divmod(s, 4)
+            if s // 2 not in ws_b:
+                ws_b.update({s // 2: keep([P, 2 * 512], BF16, f"ws_b{s // 2}", tag=tag)})
             copy(
-                out=ws_b[a][:, 512 * t : 512 * (t + 1)].rearrange("p (q i e j) -> p q i j e", q=16, e=4, j=4),
+                out=ws_b[s // 2][:, 512 * (s % 2) : 512 * (s % 2 + 1)].rearrange("p (q i e j) -> p q i j e", q=16, e=4, j=4),
                 in_=ws_raw[a][:].rearrange("p j (q t i e) -> p t q i j e", t=4, i=2, e=4)[:, t],
             )
 
@@ -138,10 +145,9 @@ def tile_list_lint_autofix_edits_kernel(
             nc.vector.quantize_mx(out=words.bitcast(FP8X4), scales=plane, in_=src)
 
         def quantize_ws(s0, s1, tag=""):
-            a, t = divmod(s0, 4)
             words = keep([P, P * (s1 - s0)], U32, f"ws_w{s0}", tag=tag)
             plane = keep([P, P * (s1 - s0)], U8, f"ws_s{s0}")
-            quantize(words[:], plane[:], ws_b[a][:, 512 * t : 512 * (t + s1 - s0)])
+            quantize(words[:], plane[:], ws_b[s0 // 2][:])
             for s in range(s0, s1):
                 cols = slice(P * (s - s0), P * (s - s0 + 1))
                 ws_q.update({s: (words[:, cols], plane[:, cols])})
@@ -165,6 +171,8 @@ def tile_list_lint_autofix_edits_kernel(
             in_=w8_w_raw[0][:].rearrange("p (q t i) -> p q t i", t=4, q=16)[:, :, 1:4, :],
         )
         quantize_ws(2, 4, tag="w8_s_raw")
+        for s in range(4, 6):
+            round_ws(s, nc.vector.tensor_copy)
 
         x1 = {}
         x2 = {}
@@ -256,12 +264,11 @@ def tile_list_lint_autofix_edits_kernel(
         shift_side(0, [(0, J)])
         make_x1(2)
         scale_side(2)
-        ws_b.update({1: keep([P, 4 * 512], BF16, "ws_b1", tag="b_0")})
-        for s in range(4, SLICES):
-            round_ws(s, nc.scalar.copy)
+        for s in range(6, SLICES):
+            round_ws(s, nc.scalar.copy, tag="b_0")
+        quantize_ws(4, 6, tag="x2_0")
         shift_side(1, [(0, J)])
-        quantize_ws(4, 8)
-        reorder(w8_w[1][:], w8_w_raw[1][:], 1)
+        quantize_ws(6, 8)
         make_x1(3)
         scale_side(3)
         make_x2(3)
@@ -282,8 +289,7 @@ def tile_list_lint_autofix_edits_kernel(
             if s == 4:
                 z0_b = apply_gain(0, 0, J)
             if s == 5:
-                round_wo(1, nc.scalar.copy, 0, 256)
-                round_wo(1, nc.vector.tensor_copy, 256, N)
+                round_wo(1, nc.scalar.copy)
             if s > 4:
                 make_x2(s)
             shift_side(s, [(0, J)] if s + 1 < SLICES else TAIL)

@@ -273,7 +273,8 @@ def tile_list_lint_autofix_edits_kernel(
         scale_side(3)
         make_x2(3)
         shift_side(2, [(0, J)])
-        round_wo(0, nc.vector.tensor_copy)
+        round_wo(0, nc.vector.tensor_copy, 0, 384)
+        round_wo(0, nc.scalar.copy, 384, N)
         shift_side(3, [(0, J)])
         quantize_wo(0)
         make_x1(4)
@@ -295,15 +296,29 @@ def tile_list_lint_autofix_edits_kernel(
             shift_side(s, [(0, J)] if s + 1 < SLICES else TAIL)
             if s == 5:
                 quantize_wo(1)
+
+        def gain_on_scalar(s, j0, j1):
+            a, t = divmod(s, 4)
+            nc.scalar.activation(out=u[a][:, t, j0:j1], in_=u[a][:, t, j0:j1], func=ACT.Copy, scale=late_cols[:, a, t : t + 1])
+
+        def round_z(a, j0, j1):
+            z_b = keep([P, 4 * (j1 - j0)], BF16, f"z_b{a}_{j0}")
+            nc.vector.tensor_copy(
+                out=z_b[:].rearrange("p (c i t) -> p c t i", t=4, i=4),
+                in_=u[a][:, :, j0:j1].rearrange("p t (c i) -> p c t i", i=4),
+            )
+            return z_b
+
         for s in range(4, SLICES - 1):
             tanh(s, 0, J)
+            gain_on_scalar(s, TAIL[WHOLE][0], J)
 
         z0 = quantize_z(z0_b, "0", tag="x1_7")
 
-        banks = [[work_bank()] * 2 for piece in range(WHOLE)] + [[work_bank("shift"), work_bank(tag)] for tag in ("scale", "shift")]
+        banks = [[work_bank()] * 2 for piece in range(len(TAIL) - 1)] + [[work_bank("shift") for pair in range(2)]]
 
         def second_stage(a, piece, words, plane):
-            split = piece >= WHOLE
+            split = piece == len(TAIL) - 1
             for nt in range(4):
                 first = nt % 2 == 0 if split else nt == 0
                 last = nt % 2 == 1 if split else nt == 3
@@ -311,34 +326,38 @@ def tile_list_lint_autofix_edits_kernel(
 
         for piece, (j0, j1) in enumerate(TAIL):
             second_stage(0, piece, z0[0][:, j0:j1], z0[1][:, j0:j1])
-        for j0, j1 in TAIL:
+        for piece, (j0, j1) in enumerate(TAIL):
             tanh(SLICES - 1, j0, j1)
+            if piece >= WHOLE:
+                gain_on_scalar(SLICES - 1, j0, j1)
         z_b = [apply_gain(1, *TAIL[0])]
         z1 = []
         for piece in range(len(TAIL)):
             if piece + 1 < len(TAIL):
-                z_b.append(apply_gain(1, *TAIL[piece + 1]))
+                z_b.append((apply_gain if piece + 1 < WHOLE else round_z)(1, *TAIL[piece + 1]))
             z1.append(quantize_z(z_b[piece], f"1_{piece}"))
 
         def add_bias(res, acc, nt):
             nc.scalar.activation(out=res, in_=acc, func=ACT.Identity, bias=late_cols[:, 0, 4 + nt : 5 + nt])
 
-        for piece, (j0, j1) in enumerate(TAIL):
+        def finish(piece, nt0, nt1, on_scalar, queue):
+            j0, j1 = TAIL[piece]
+            acc = banks[piece][nt0 // 2][:, P * nt0 : P * nt1].rearrange("p (e j) -> p e j", j=P)
+            res = keep([P, nt1 - nt0, P], F32, f"res{piece}_{nt0}")
+            if on_scalar:
+                for nt in range(nt0, nt1):
+                    add_bias(res[:, nt - nt0, :], acc[:, nt - nt0, :], nt)
+            else:
+                nc.vector.tensor_tensor(res[:], acc, late_cols[:, 0, 4 + nt0 : 4 + nt1].unsqueeze(2).to_broadcast([P, nt1 - nt0, P]), ALU.add)
+            queue.dma_start(out=out_rows[:, nt0:nt1, j0:j1], in_=res[:])
+
+        for piece in range(len(TAIL)):
             second_stage(1, piece, z1[piece][0][:], z1[piece][1][:])
             if piece < WHOLE:
-                res = keep([P, 4, P], F32, f"res{piece}")
-                for nt in range(4):
-                    add_bias(res[:, nt, :], banks[piece][0][:, P * nt : P * (nt + 1)], nt)
-                nc.sync.dma_start(out=out_rows[:, :, j0:j1], in_=res[:])
+                finish(piece, 0, 2, True, nc.sync)
+                finish(piece, 2, 4, True, nc.sync)
+            elif piece + 1 < len(TAIL):
+                finish(piece, 0, 4, False, nc.sync)
             else:
-                res = [keep([P, 2, P], F32, f"res{piece}_{pair}") for pair in range(2)]
-                for nt in range(2):
-                    add_bias(res[0][:, nt, :], banks[piece][0][:, P * nt : P * (nt + 1)], nt)
-                nc.scalar.dma_start(out=out_rows[:, 0:2, j0:j1], in_=res[0][:])
-                nc.vector.tensor_tensor(
-                    res[1][:],
-                    banks[piece][1][:, 2 * P : 4 * P].rearrange("p (e j) -> p e j", e=2),
-                    late_cols[:, 0, 6:8].unsqueeze(2).to_broadcast([P, 2, P]),
-                    ALU.add,
-                )
-                nc.sync.dma_start(out=out_rows[:, 2:4, j0:j1], in_=res[1][:])
+                finish(piece, 0, 2, True, nc.scalar)
+                finish(piece, 2, 4, False, nc.sync)

@@ -273,8 +273,7 @@ def tile_list_lint_autofix_edits_kernel(
         scale_side(3)
         make_x2(3)
         shift_side(2, [(0, J)])
-        round_wo(0, nc.vector.tensor_copy, 0, 384)
-        round_wo(0, nc.scalar.copy, 384, N)
+        round_wo(0, nc.vector.tensor_copy)
         shift_side(3, [(0, J)])
         quantize_wo(0)
         make_x1(4)
@@ -311,7 +310,6 @@ def tile_list_lint_autofix_edits_kernel(
 
         for s in range(4, SLICES - 1):
             tanh(s, 0, J)
-            gain_on_scalar(s, TAIL[WHOLE][0], J)
 
         z0 = quantize_z(z0_b, "0", tag="x1_7")
 
@@ -328,6 +326,9 @@ def tile_list_lint_autofix_edits_kernel(
             second_stage(0, piece, z0[0][:, j0:j1], z0[1][:, j0:j1])
         for piece, (j0, j1) in enumerate(TAIL):
             tanh(SLICES - 1, j0, j1)
+            if piece == WHOLE - 1:
+                for s in range(4, SLICES - 1):
+                    gain_on_scalar(s, TAIL[WHOLE][0], J)
             if piece >= WHOLE:
                 gain_on_scalar(SLICES - 1, j0, j1)
         z_b = [apply_gain(1, *TAIL[0])]

@@ -79,8 +79,8 @@ def tile_list_lint_autofix_edits_kernel(
         nc.sync.dma_start(out=tab_w[:].bitcast(I32), in_=tab_words[0].rearrange("p t i -> p (t i)").bitcast(I32))
         nc.sync.dma_start(offs2_t[:], offs2)
         load_plane(nc.sync, w4_s_raw[:], w4_scales)
-        nc.sync.dma_start(out=rows[0][0:4, :].rearrange("t (g i) -> t g i", i=8), in_=bs.rearrange(by_slot, t=4, i=8))
         nc.sync.dma_start(out=ws_raw[0][:], in_=ws_rows[:, :, 0:512])
+        nc.sync.dma_start(out=rows[0][0:4, :].rearrange("t (g i) -> t g i", i=8), in_=bs.rearrange(by_slot, t=4, i=8))
         load_plane(nc.sync, tab2_s[:], tab2_scales)
         nc.sync.dma_start(out=tab2_w[:].bitcast(I32), in_=tab2_words[0].rearrange("p t i -> p (t i)").bitcast(I32))
         nc.sync.dma_start(out=w8_w_raw[0][:], in_=w8_rows[:, 0:512])

@@ -126,8 +126,8 @@ def tile_list_lint_autofix_edits_kernel(
         ws_b = {}
         ws_q = {}
 
-        def reorder(dst, src, groups):
-            nc.vector.tensor_copy(
+        def reorder(dst, src, groups, engine=nc.vector):
+            engine.tensor_copy(
                 out=dst.rearrange("p (a t q i) -> p a q t i", a=groups, t=4, q=16),
                 in_=src.rearrange("p (a q t i) -> p a q t i", a=groups, t=4, q=16),
             )
@@ -152,11 +152,11 @@ def tile_list_lint_autofix_edits_kernel(
                 cols = slice(P * (s - s0), P * (s - s0 + 1))
                 ws_q.update({s: (words[:, cols], plane[:, cols])})
 
-        reorder(w4_w[:].bitcast(I32), w4_w_raw[:].bitcast(I32), PASSES)
+        reorder(w4_w[:].bitcast(I32), w4_w_raw[:].bitcast(I32), PASSES, nc.gpsimd)
         nc.vector.tensor_copy(out=v_s[:], in_=tab_s[:].indirect(offs_t[:]))
         nc.vector.tensor_copy(out=v_w[0][:], in_=tab_w[:].indirect(offs_t[:, 0:32]))
-        reorder(w4_s[:].bitcast(I32), w4_s_raw[:].bitcast(I32), PASSES)
-        v_w.append(keep([P, BANK], U32, "v_w1", tag="w4_s_raw"))
+        reorder(w4_s[:].bitcast(I32), w4_s_raw[:].bitcast(I32), PASSES, nc.gpsimd)
+        v_w.append(keep([P, BANK], U32, "v_w1"))
         nc.vector.tensor_copy(out=v_w[1][:], in_=tab_w[:].indirect(offs_t[:, 32:64]))
         for s in range(4):
             round_ws(s, nc.vector.tensor_copy)

@@ -75,7 +75,8 @@ def tile_list_lint_autofix_edits_kernel(
         by_slot = "(g t i) -> t g i"
         nc.sync.dma_start(offs_t[:], offs)
         nc.sync.dma_start(out=w4_w_raw[:].bitcast(I32), in_=w4_words[0].bitcast(I32))
-        load_plane(nc.sync, tab_s[:], tab_scales)
+        load_plane(nc.sync, tab_s[:], tab_scales, range(2))
+        load_plane(nc.scalar, tab_s[:], tab_scales, range(2, 4))
         nc.sync.dma_start(out=tab_w[:].bitcast(I32), in_=tab_words[0].rearrange("p t i -> p (t i)").bitcast(I32))
         nc.sync.dma_start(offs2_t[:], offs2)
         load_plane(nc.sync, w4_s_raw[:], w4_scales)
@@ -163,10 +164,10 @@ def tile_list_lint_autofix_edits_kernel(
         quantize_ws(0, 2)
         nc.vector.tensor_copy(out=v2_s[:], in_=tab2_s[:].indirect(offs2_t[:]))
         nc.vector.tensor_copy(out=v2_w[:], in_=tab2_w[:].indirect(offs2_t[:]))
-        reorder(w8_s[:].bitcast(I32), w8_s_raw[:].bitcast(I32), PASSES)
+        reorder(w8_s[:].bitcast(I32), w8_s_raw[:].bitcast(I32), PASSES, nc.gpsimd)
         by_slice = w8_w_raw[0][:].rearrange("p (q t i) -> p t q i", t=4, q=16)
-        nc.vector.tensor_copy(out=w8_first[:].rearrange("p (q i) -> p q i", q=16), in_=by_slice[:, 0])
-        nc.vector.tensor_copy(
+        nc.gpsimd.tensor_copy(out=w8_first[:].rearrange("p (q i) -> p q i", q=16), in_=by_slice[:, 0])
+        nc.gpsimd.tensor_copy(
             out=w8_w[0][:, P:512].rearrange("p (t q i) -> p q t i", t=3, q=16),
             in_=w8_w_raw[0][:].rearrange("p (q t i) -> p q t i", t=4, q=16)[:, :, 1:4, :],
         )
@@ -197,7 +198,7 @@ def tile_list_lint_autofix_edits_kernel(
             a, t = divmod(s, 4)
             words = w8_first[:] if s == 0 else w8_w[a][:, P * t : P * (t + 1)]
             bank = product(words.bitcast(FP8X4), w8_s[:, P * s : P * (s + 1)], v2_w[:], v2_s[:], "proj")
-            nc.scalar.copy(out=b[s][:], in_=bank[:])
+            (nc.vector.tensor_copy if s == 0 else nc.scalar.copy)(out=b[s][:], in_=bank[:])
             scaled[s] = ring.tile([P, J], F32, name="scaled")
             nc.vector.tensor_tensor(scaled[s][:], x1[s][:].indirect(pos_t[:]), b[s][:], ALU.mult)
 

@@ -22,7 +22,10 @@ BANK = 512
 SLICES = H // P
 PASSES = H // 512
 TAIL = [(j0, j0 + P) for j0 in range(0, J, P)]
-WHOLE = 2
+WHOLE = 1
+X1_BANKS = [("S1", "S2"), ("S0", "X"), ("P1", "P0"), ("S1", "S2"), ("S0", "X"), ("S1", "S2"), ("S0", "X"), ("S1", "S2")]
+X2_BANKS = [("X", "X"), ("H0", "H1"), ("H0", "H0")] + [("H1", "H0")] * 5
+B_BANKS = ["P1", "P0", "S1", "S2", "P1", "P1", "P0", "P1"]
 
 
 def tile_list_lint_autofix_edits_kernel(
@@ -38,8 +41,10 @@ def tile_list_lint_autofix_edits_kernel(
         def keep(shape, dtype, name, tag=""):
             return held.tile(shape, dtype, name=name, tag=tag, align_bytes=64)
 
-        def work_bank(tag="scale"):
-            return psum.tile([P, BANK], F32, name="work", tag=tag, bufs=2 if tag == "proj" else 3)
+        psum_banks = {tag: psum.tile([P, BANK], F32, name=tag, tag=tag) for tag in ("S0", "S1", "S2", "X", "H0", "H1", "P0", "P1")}
+
+        def work_bank(tag):
+            return psum_banks[tag]
 
         def load_plane(queue, plane, rows, quadrants=range(4)):
             for q in quadrants:
@@ -50,7 +55,7 @@ def tile_list_lint_autofix_edits_kernel(
         offs2_t = held.tile([P, J // 16], U16, name="offs2_t")
         tab_w = keep([P, T], U32, "tab_w")
         tab_s = keep([P, T], U8, "tab_s")
-        tab2_w = keep([P, T2], U32, "tab2_w")
+        tab2_w = keep([P, T2], U32, "tab2_w", tag="tab2_w")
         tab2_s = keep([P, T2], U8, "tab2_s")
         w8_s_raw = keep([P, H], U8, "w8_s_raw", tag="w8_s_raw")
         w4_s_raw = keep([P, H], U8, "w4_s_raw", tag="w4_s_raw")
@@ -68,7 +73,7 @@ def tile_list_lint_autofix_edits_kernel(
         ws_rows = ws.rearrange("(p j) r -> p j r", j=4)
         ws_raw = [keep([P, 4, 512], F32, f"ws_raw{a}") for a in range(PASSES)]
         wo_raw = [keep([P, 4, N], F32, f"wo_raw{a}") for a in range(PASSES)]
-        w8_w_raw = [keep([P, 512], I32, "w8_w_raw0")]
+        w8_w_raw = [keep([P, 512], I32, "w8_w_raw0", tag="w8_w_raw0")]
         w4_w_raw = keep([P, 2 * H], U8, "w4_w_raw")
         w8_rows = w8_words[0].rearrange("p c i -> p (c i)").bitcast(I32)
 
@@ -84,8 +89,8 @@ def tile_list_lint_autofix_edits_kernel(
         nc.sync.dma_start(out=rows[0][0:4, :].rearrange("t (g i) -> t g i", i=8), in_=bs.rearrange(by_slot, t=4, i=8))
         load_plane(nc.sync, tab2_s[:], tab2_scales)
         nc.sync.dma_start(out=tab2_w[:].bitcast(I32), in_=tab2_words[0].rearrange("p t i -> p (t i)").bitcast(I32))
-        nc.sync.dma_start(out=w8_w_raw[0][:], in_=w8_rows[:, 0:512])
         load_plane(nc.sync, w8_s_raw[:], w8_scales)
+        nc.sync.dma_start(out=w8_w_raw[0][:], in_=w8_rows[:, 0:512])
         wo_rows = wo.rearrange("(a q t i) n -> a t q i n", a=PASSES, t=4, i=8)
 
         def load_wo(a):
@@ -106,7 +111,7 @@ def tile_list_lint_autofix_edits_kernel(
         load_wo(1)
 
         def onto_partitions(staged, name):
-            turned = work_bank("proj")
+            turned = work_bank("P0")
             for a in range(PASSES):
                 nc.tensor.transpose(turned[:, P * a : P * (a + 1)], staged[:, P * a : P * (a + 1)], ident[:])
             cols = keep([P, PASSES, 8], F32, name)
@@ -122,7 +127,7 @@ def tile_list_lint_autofix_edits_kernel(
         v2_s = keep([P, J], U8, "v2_s")
         w4_w = keep([P, 2 * H], U8, "w4_w")
         w8_s = keep([P, H], U8, "w8_s")
-        w8_first = keep([P, P], I32, "w8_first")
+        w8_first = keep([P, P], I32, "w8_first", tag="w8_first")
         w8_w = [keep([P, 512], I32, "w8_w0"), w8_late]
         ws_b = {}
         ws_q = {}
@@ -155,11 +160,12 @@ def tile_list_lint_autofix_edits_kernel(
 
         reorder(w4_w[:].bitcast(I32), w4_w_raw[:].bitcast(I32), PASSES, nc.gpsimd)
         nc.vector.tensor_copy(out=v_s[:], in_=tab_s[:].indirect(offs_t[:]))
-        nc.vector.tensor_copy(out=v_w[0][:], in_=tab_w[:].indirect(offs_t[:, 0:32]))
+        nc.vector.tensor_copy(out=v_w[0][:, 0:256], in_=tab_w[:].indirect(offs_t[:, 0:16]))
+        nc.vector.tensor_copy(out=v_w[0][:, 256:512], in_=tab_w[:].indirect(offs_t[:, 16:32]))
         reorder(w4_s[:].bitcast(I32), w4_s_raw[:].bitcast(I32), PASSES, nc.gpsimd)
         v_w.append(keep([P, BANK], U32, "v_w1"))
         nc.vector.tensor_copy(out=v_w[1][:], in_=tab_w[:].indirect(offs_t[:, 32:64]))
-        for s in range(4):
+        for s in range(2):
             round_ws(s, nc.vector.tensor_copy)
         quantize_ws(0, 2)
         nc.vector.tensor_copy(out=v2_s[:], in_=tab2_s[:].indirect(offs2_t[:]))
@@ -171,9 +177,9 @@ def tile_list_lint_autofix_edits_kernel(
             out=w8_w[0][:, P:512].rearrange("p (t q i) -> p q t i", t=3, q=16),
             in_=w8_w_raw[0][:].rearrange("p (q t i) -> p q t i", t=4, q=16)[:, :, 1:4, :],
         )
-        quantize_ws(2, 4, tag="w8_s_raw")
-        for s in range(4, 6):
-            round_ws(s, nc.vector.tensor_copy)
+        for s in range(2, 4):
+            round_ws(s, nc.vector.tensor_copy, tag="tab2_w")
+        quantize_ws(2, 4)
 
         x1 = {}
         x2 = {}
@@ -181,7 +187,7 @@ def tile_list_lint_autofix_edits_kernel(
         scaled = {}
         u = [keep([P, 4, J], F32, f"u_{a}") for a in range(PASSES)]
 
-        def product(lhsT, lhsT_scale, words, plane, tag="scale"):
+        def product(lhsT, lhsT_scale, words, plane, tag):
             bank = work_bank(tag)
             nc.tensor.matmul_mx(out=bank[:], lhsT=lhsT, lhsT_scale=lhsT_scale, rhs=words.bitcast(FP8X4), rhs_scale=plane, start=True, stop=True)
             return bank
@@ -191,14 +197,16 @@ def tile_list_lint_autofix_edits_kernel(
             if s not in x1:
                 x1.update({s: keep([P, S], F32, f"x1_{s}", tag=f"x1_{s}")})
             for h in halves:
-                bank = product(ws_q[s][0].bitcast(FP8X4), ws_q[s][1], v_w[h][:], v_s[:, BANK * h : BANK * (h + 1)])
+                bank = product(ws_q[s][0].bitcast(FP8X4), ws_q[s][1], v_w[h][:], v_s[:, BANK * h : BANK * (h + 1)], X1_BANKS[s][h])
                 nc.scalar.activation(out=x1[s][:, BANK * h : BANK * (h + 1)], in_=bank[:], func=ACT.Identity, bias=bs_cols[:, a, t : t + 1])
 
-        def scale_side(s):
+        def make_b(s):
             a, t = divmod(s, 4)
             words = w8_first[:] if s == 0 else w8_w[a][:, P * t : P * (t + 1)]
-            bank = product(words.bitcast(FP8X4), w8_s[:, P * s : P * (s + 1)], v2_w[:], v2_s[:], "proj")
+            bank = product(words.bitcast(FP8X4), w8_s[:, P * s : P * (s + 1)], v2_w[:], v2_s[:], B_BANKS[s])
             (nc.vector.tensor_copy if s == 0 else nc.scalar.copy)(out=b[s][:], in_=bank[:])
+
+        def pick_scale(s):
             scaled[s] = ring.tile([P, J], F32, name="scaled")
             nc.vector.tensor_tensor(scaled[s][:], x1[s][:].indirect(pos_t[:]), b[s][:], ALU.mult)
 
@@ -206,7 +214,7 @@ def tile_list_lint_autofix_edits_kernel(
             if s not in x2:
                 x2.update({s: keep([P, S], F32, f"x2_{s}", tag=f"x2_{s}" if s < 3 else f"x1_{s - 3}")})
             for h in halves:
-                bank = product(w4_w[:, 2 * P * s : 2 * P * (s + 1)].bitcast(FP4X4), w4_s[:, P * s : P * (s + 1)], v_w[h][:], v_s[:, BANK * h : BANK * (h + 1)], "shift")
+                bank = product(w4_w[:, 2 * P * s : 2 * P * (s + 1)].bitcast(FP4X4), w4_s[:, P * s : P * (s + 1)], v_w[h][:], v_s[:, BANK * h : BANK * (h + 1)], X2_BANKS[s][h])
                 nc.scalar.copy(out=x2[s][:, BANK * h : BANK * (h + 1)], in_=bank[:])
 
         def shift_side(s, pieces):
@@ -236,11 +244,13 @@ def tile_list_lint_autofix_edits_kernel(
             quantize(z_w[:], z_s[:], z_b[:])
             return z_w, z_s
 
-        wo_b = [keep([P, 4 * N], BF16, f"wo_b{a}") for a in range(PASSES)]
+        wo_b = {}
         wo_w = keep([P, PASSES * N], U32, "wo_w")
         wo_s = keep([P, PASSES * N], U8, "wo_s")
 
         def round_wo(a, copy, n0=0, n1=N):
+            if a not in wo_b:
+                wo_b.update({a: keep([P, 4 * N], BF16, f"wo_b{a}", tag="x2_2" if a == 0 else "b_4")})
             copy(
                 out=wo_b[a][:, 4 * n0 : 4 * n1].rearrange("p (c i t) -> p c t i", t=4, i=4),
                 in_=wo_raw[a][:, :, n0:n1].rearrange("p t (c i) -> p c t i", i=4),
@@ -255,44 +265,64 @@ def tile_list_lint_autofix_edits_kernel(
 
         out_rows = out.rearrange("(b p) j -> p b j", p=P)
 
-        for h in range(2):
-            for s in range(3):
-                make_x2(s, [h])
+        for c0, tags in ((0, ("X", "H0")), (256, ("H1", "S0"))):
+            for s in range(2):
+                if s not in x2:
+                    x2.update({s: keep([P, S], F32, f"x2_{s}", tag=f"x2_{s}")})
+                bank = work_bank(tags[s])
+                nc.tensor.matmul_mx(
+                    out=bank[:, 0:256], lhsT=w4_w[:, 2 * P * s : 2 * P * (s + 1)].bitcast(FP4X4), lhsT_scale=w4_s[:, P * s : P * (s + 1)],
+                    rhs=v_w[0][:, c0 : c0 + 256].bitcast(FP8X4), rhs_scale=v_s[:, c0 : c0 + 256], start=True, stop=True,
+                )
+                nc.scalar.copy(out=x2[s][:, c0 : c0 + 256], in_=bank[:, 0:256])
+        make_x2(2, [0])
+        for s in range(3):
+            make_x2(s, [1])
         make_x1(0)
         make_x1(1)
-        scale_side(0)
-        scale_side(1)
+        make_b(0)
+        for s in range(4, 6):
+            round_ws(s, nc.vector.tensor_copy)
+        make_b(1)
+        make_b(2)
+        make_b(3)
+        pick_scale(0)
+        pick_scale(1)
         shift_side(0, [(0, J)])
+        quantize_ws(4, 6, tag="b_1")
         make_x1(2)
-        scale_side(2)
+        pick_scale(2)
         for s in range(6, SLICES):
             round_ws(s, nc.scalar.copy, tag="b_0")
-        quantize_ws(4, 6, tag="x2_0")
         shift_side(1, [(0, J)])
         quantize_ws(6, 8)
         make_x1(3)
-        scale_side(3)
+        pick_scale(3)
         make_x2(3)
         shift_side(2, [(0, J)])
         round_wo(0, nc.vector.tensor_copy)
         shift_side(3, [(0, J)])
         quantize_wo(0)
         make_x1(4)
-        scale_side(4)
+        make_b(4)
+        pick_scale(4)
         make_x2(4)
         late_cols = onto_partitions(rows[1], "late_cols")
-        for s in range(4):
-            tanh(s, 0, J)
         for s in range(4, SLICES):
             if s + 1 < SLICES:
                 make_x1(s + 1)
-                scale_side(s + 1)
+                make_b(s + 1)
+                pick_scale(s + 1)
             if s == 4:
+                for early in range(4):
+                    tanh(early, 0, J)
                 z0_b = apply_gain(0, 0, J)
             if s == 5:
                 round_wo(1, nc.scalar.copy)
             if s > 4:
                 make_x2(s)
+            if s == SLICES - 1:
+                z0 = quantize_z(z0_b, "0", tag="x1_3")
             shift_side(s, [(0, J)] if s + 1 < SLICES else TAIL)
             if s == 5:
                 quantize_wo(1)
@@ -309,12 +339,14 @@ def tile_list_lint_autofix_edits_kernel(
             )
             return z_b
 
-        for s in range(4, SLICES - 1):
+        for s in range(4, 6):
             tanh(s, 0, J)
+        for s in range(4, 6):
+            gain_on_scalar(s, TAIL[WHOLE][0], J)
+        tanh(6, 0, J)
 
-        z0 = quantize_z(z0_b, "0", tag="x1_7")
 
-        banks = [[work_bank()] * 2 for piece in range(len(TAIL) - 1)] + [[work_bank("shift") for pair in range(2)]]
+        banks = [[work_bank(tag)] * 2 for tag in ("S0", "X", "S1")] + [[work_bank("H1"), work_bank("H0")]]
 
         def second_stage(a, piece, words, plane):
             split = piece == len(TAIL) - 1
@@ -328,8 +360,7 @@ def tile_list_lint_autofix_edits_kernel(
         for piece, (j0, j1) in enumerate(TAIL):
             tanh(SLICES - 1, j0, j1)
             if piece == WHOLE - 1:
-                for s in range(4, SLICES - 1):
-                    gain_on_scalar(s, TAIL[WHOLE][0], J)
+                gain_on_scalar(SLICES - 2, TAIL[WHOLE][0], J)
             if piece >= WHOLE:
                 gain_on_scalar(SLICES - 1, j0, j1)
         z_b = [apply_gain(1, *TAIL[0])]
@@ -355,7 +386,7 @@ def tile_list_lint_autofix_edits_kernel(
 
         for piece in range(len(TAIL)):
             second_stage(1, piece, z1[piece][0][:], z1[piece][1][:])
-            if piece < WHOLE:
+            if piece < 2:
                 finish(piece, 0, 2, True, nc.sync)
                 finish(piece, 2, 4, True, nc.sync)
             elif piece + 1 < len(TAIL):

@@ -22,7 +22,7 @@ BANK = 512
 SLICES = H // P
 PASSES = H // 512
 TAIL = [(j0, j0 + P) for j0 in range(0, J, P)]
-WHOLE = 1
+WHOLE = 2
 X1_BANKS = [("S1", "S2"), ("S0", "X"), ("P1", "P0"), ("S1", "S2"), ("S0", "X"), ("S1", "S2"), ("S0", "X"), ("S1", "S2")]
 X2_BANKS = [("X", "X"), ("H0", "H1"), ("H0", "H0")] + [("H1", "H0")] * 5
 B_BANKS = ["P1", "P0", "S1", "S2", "P1", "P1", "P0", "P1"]
@@ -226,6 +226,10 @@ def tile_list_lint_autofix_edits_kernel(
             a, t = divmod(s, 4)
             nc.scalar.activation(out=u[a][:, t, j0:j1], in_=u[a][:, t, j0:j1], func=ACT.Tanh)
 
+        def tanh_pair(s):
+            a, t = divmod(s, 4)
+            nc.scalar.activation(out=u[a][:, t : t + 2, :], in_=u[a][:, t : t + 2, :], func=ACT.Tanh)
+
         def apply_gain(a, j0, j1):
             width = j1 - j0
             z_b = keep([P, 4 * width], BF16, f"z_b{a}_{j0}")
@@ -314,8 +318,8 @@ def tile_list_lint_autofix_edits_kernel(
                 make_b(s + 1)
                 pick_scale(s + 1)
             if s == 4:
-                for early in range(4):
-                    tanh(early, 0, J)
+                for early in range(0, 4, 2):
+                    tanh_pair(early)
                 z0_b = apply_gain(0, 0, J)
             if s == 5:
                 round_wo(1, nc.scalar.copy)
@@ -339,8 +343,7 @@ def tile_list_lint_autofix_edits_kernel(
             )
             return z_b
 
-        for s in range(4, 6):
-            tanh(s, 0, J)
+        tanh_pair(4)
         for s in range(4, 6):
             gain_on_scalar(s, TAIL[WHOLE][0], J)
         tanh(6, 0, J)
@@ -386,7 +389,7 @@ def tile_list_lint_autofix_edits_kernel(
 
         for piece in range(len(TAIL)):
             second_stage(1, piece, z1[piece][0][:], z1[piece][1][:])
-            if piece < 2:
+            if piece < WHOLE:
                 finish(piece, 0, 2, True, nc.sync)
                 finish(piece, 2, 4, True, nc.sync)
             elif piece + 1 < len(TAIL):

@@ -24,8 +24,9 @@ PASSES = H // 512
 TAIL = [(j0, j0 + P) for j0 in range(0, J, P)]
 WHOLE = 2
 X1_BANKS = [("S1", "S2"), ("S0", "X"), ("P1", "P0"), ("S1", "S2"), ("S0", "X"), ("S1", "S2"), ("S0", "X"), ("S1", "S2")]
-X2_BANKS = [("X", "X"), ("H0", "H1"), ("H0", "H0")] + [("H1", "H0")] * 5
-B_BANKS = ["P1", "P0", "S1", "S2", "P1", "P1", "P0", "P1"]
+X2_BANKS = [("X", "X"), ("H0", "H1"), ("H0", "H0"), ("H1", "H0"), ("H1", "P1")] + [("H1", "H0")] * 3
+B_BANKS = ["P1", "P0", "S1", "S2", "P1", "P1", "H0", "P0"]
+POOL_COLS = 128
 
 
 def tile_list_lint_autofix_edits_kernel(
@@ -116,9 +117,9 @@ def tile_list_lint_autofix_edits_kernel(
                 nc.tensor.transpose(turned[:, P * a : P * (a + 1)], staged[:, P * a : P * (a + 1)], ident[:])
             cols = keep([P, PASSES, 8], F32, name)
             nc.scalar.copy(out=cols[:], in_=turned[:, 0 : 2 * P].rearrange("p (a c) -> p a c", a=PASSES)[:, :, 0:8])
-            return cols
+            return cols, turned
 
-        bs_cols = onto_partitions(rows[0], "bs_cols")
+        bs_cols, bs_bank = onto_partitions(rows[0], "bs_cols")
 
         v_w = [keep([P, BANK], U32, "v_w0")]
         w4_s = keep([P, H], U8, "w4_s")
@@ -185,7 +186,7 @@ def tile_list_lint_autofix_edits_kernel(
         x2 = {}
         b = [keep([P, J], F32, f"b_{s}", tag=f"b_{s}") for s in range(SLICES)]
         scaled = {}
-        u = [keep([P, 4, J], F32, f"u_{a}") for a in range(PASSES)]
+        u = [keep([P, 4, J], F32, f"u_{a}", tag=f"u_{a}") for a in range(PASSES)]
 
         def product(lhsT, lhsT_scale, words, plane, tag):
             bank = work_bank(tag)
@@ -236,7 +237,7 @@ def tile_list_lint_autofix_edits_kernel(
             nc.vector.tensor_tensor(
                 z_b[:].rearrange("p (c i t) -> p c t i", t=4, i=4),
                 u[a][:, :, j0:j1].rearrange("p t (c i) -> p c t i", i=4),
-                late_cols[:, a, 0:4].unsqueeze(1).unsqueeze(3).to_broadcast([P, width // 4, 4, 4]),
+                (late_bank[:, 0:4] if a == 0 else late_cols[:, a, 0:4]).unsqueeze(1).unsqueeze(3).to_broadcast([P, width // 4, 4, 4]),
                 ALU.mult,
             )
             return z_b
@@ -265,7 +266,7 @@ def tile_list_lint_autofix_edits_kernel(
 
         def second_pass(acc, a, nt, words, plane, start, stop):
             cols = slice(N * a + P * nt, N * a + P * (nt + 1))
-            nc.tensor.matmul_mx(out=acc, lhsT=wo_w[:, cols].bitcast(FP8X4), lhsT_scale=wo_s[:, cols], rhs=words.bitcast(FP8X4), rhs_scale=plane, start=start, stop=stop)
+            nc.tensor.matmul_mx(out=acc, lhsT=(wo_w_first[:] if a == 0 and nt == 0 else wo_w[:, cols]).bitcast(FP8X4), lhsT_scale=wo_s[:, cols], rhs=words.bitcast(FP8X4), rhs_scale=plane, start=start, stop=stop)
 
         out_rows = out.rearrange("(b p) j -> p b j", p=P)
 
@@ -304,30 +305,40 @@ def tile_list_lint_autofix_edits_kernel(
         pick_scale(3)
         make_x2(3)
         shift_side(2, [(0, J)])
-        round_wo(0, nc.vector.tensor_copy)
+        round_wo(0, nc.vector.tensor_copy, POOL_COLS, N)
         shift_side(3, [(0, J)])
-        quantize_wo(0)
+        quantize(wo_w[:, POOL_COLS:N], wo_s[:, POOL_COLS:N], wo_b[0][:, 4 * POOL_COLS : 4 * N])
         make_x1(4)
         make_b(4)
         pick_scale(4)
-        make_x2(4)
-        late_cols = onto_partitions(rows[1], "late_cols")
+        late_cols, late_bank = onto_partitions(rows[1], "late_cols")
         for s in range(4, SLICES):
             if s + 1 < SLICES:
                 make_x1(s + 1)
                 make_b(s + 1)
                 pick_scale(s + 1)
             if s == 4:
+                make_x2(4)
                 for early in range(0, 4, 2):
                     tanh_pair(early)
+                shift_side(4, [(0, J)])
                 z0_b = apply_gain(0, 0, J)
+                wo_b_first = keep([P, 4 * POOL_COLS], BF16, "wo_b_first", tag="x1_1")
+                nc.gpsimd.tensor_copy(
+                    out=wo_b_first[:].rearrange("p (n t) -> p n t", t=4),
+                    in_=wo_raw[0][:, :, 0:POOL_COLS].rearrange("p t n -> p n t"),
+                )
             if s == 5:
                 round_wo(1, nc.scalar.copy)
             if s > 4:
                 make_x2(s)
             if s == SLICES - 1:
                 z0 = quantize_z(z0_b, "0", tag="x1_3")
-            shift_side(s, [(0, J)] if s + 1 < SLICES else TAIL)
+            if s == 5:
+                wo_w_first = keep([P, POOL_COLS], U32, "wo_w_first", tag="u_0")
+                quantize(wo_w_first[:], wo_s[:, 0:POOL_COLS], wo_b_first[:])
+            if s > 4:
+                shift_side(s, [(0, J)] if s + 1 < SLICES else TAIL)
             if s == 5:
                 quantize_wo(1)
 

@@ -26,7 +26,7 @@ WHOLE = 2
 X1_BANKS = [("S1", "S2"), ("S0", "X"), ("P1", "P0"), ("S1", "S2"), ("S0", "X"), ("S1", "S2"), ("S0", "X"), ("S1", "S2")]
 X2_BANKS = [("X", "X"), ("H0", "H1"), ("H0", "H0"), ("H1", "H0"), ("H1", "P1")] + [("H1", "H0")] * 3
 B_BANKS = ["P1", "P0", "S1", "S2", "P1", "P1", "H0", "P0"]
-POOL_COLS = 128
+POOL_COLS = 256
 
 
 def tile_list_lint_autofix_edits_kernel(
@@ -266,7 +266,7 @@ def tile_list_lint_autofix_edits_kernel(
 
         def second_pass(acc, a, nt, words, plane, start, stop):
             cols = slice(N * a + P * nt, N * a + P * (nt + 1))
-            nc.tensor.matmul_mx(out=acc, lhsT=(wo_w_first[:] if a == 0 and nt == 0 else wo_w[:, cols]).bitcast(FP8X4), lhsT_scale=wo_s[:, cols], rhs=words.bitcast(FP8X4), rhs_scale=plane, start=start, stop=stop)
+            nc.tensor.matmul_mx(out=acc, lhsT=(wo_w_first[:, cols] if a == 0 and P * nt < POOL_COLS else wo_w[:, cols]).bitcast(FP8X4), lhsT_scale=wo_s[:, cols], rhs=words.bitcast(FP8X4), rhs_scale=plane, start=start, stop=stop)
 
         out_rows = out.rearrange("(b p) j -> p b j", p=P)
 
@@ -323,7 +323,7 @@ def tile_list_lint_autofix_edits_kernel(
                     tanh_pair(early)
                 shift_side(4, [(0, J)])
                 z0_b = apply_gain(0, 0, J)
-                wo_b_first = keep([P, 4 * POOL_COLS], BF16, "wo_b_first", tag="x1_1")
+                wo_b_first = keep([P, 4 * POOL_COLS], BF16, "wo_b_first", tag="x1_5")
                 nc.gpsimd.tensor_copy(
                     out=wo_b_first[:].rearrange("p (n t) -> p n t", t=4),
                     in_=wo_raw[0][:, :, 0:POOL_COLS].rearrange("p t n -> p n t"),

from contextlib import ExitStack

import concourse.mybir as mybir
from concourse.masks import make_identity

K, H, N, T, S, T2, J = 512, 1024, 512, 2048, 1024, 2048, 512
FLOPS = 2 * K * H * S * 2 + 2 * K * H * J + 2 * H * N * J

F32 = mybir.dt.float32
BF16 = mybir.dt.bfloat16
I32 = mybir.dt.int32
U32 = mybir.dt.uint32
U16 = mybir.dt.uint16
U8 = mybir.dt.uint8
FP8X4 = mybir.dt.float8_e4m3fn_x4
FP4X4 = mybir.dt.float4_e2m1fn_x4
ACT = mybir.ActivationFunctionType
ALU = mybir.AluOpType

P = 128
BANK = 512
SLICES = H // P
PASSES = H // 512
TAIL = [(j0, j0 + P) for j0 in range(0, J, P)]
WHOLE = 2
X1_BANKS = [("S1", "S2"), ("S0", "X"), ("P1", "P0"), ("S1", "S2"), ("S0", "X"), ("S1", "S2"), ("S0", "X"), ("S1", "S2")]
X2_BANKS = [("X", "X"), ("H0", "H1"), ("H0", "H0"), ("H1", "H0"), ("H1", "P1")] + [("H1", "H0")] * 3
B_BANKS = ["P1", "P0", "S1", "S2", "P1", "P1", "H0", "P0"]
POOL_COLS = 256


def tile_list_lint_autofix_edits_kernel(
    tc, tab_words, tab_scales, tab2_words, tab2_scales, offs, pos1, offs2, ws, bs,
    w4_words, w4_scales, w8_words, w8_scales, gain, wo, bo, out,
):
    nc = tc.nc
    with ExitStack() as ctx:
        held = ctx.enter_context(tc.tile_pool(name="held", bufs=1))
        ring = ctx.enter_context(tc.tile_pool(name="ring", bufs=4))
        psum = ctx.enter_context(tc.psum_pool(name="psum", bufs=1))

        def keep(shape, dtype, name, tag=""):
            return held.tile(shape, dtype, name=name, tag=tag, align_bytes=64)

        psum_banks = {tag: psum.tile([P, BANK], F32, name=tag, tag=tag) for tag in ("S0", "S1", "S2", "X", "H0", "H1", "P0", "P1")}

        def work_bank(tag):
            return psum_banks[tag]

        def load_plane(queue, plane, rows, quadrants=range(4)):
            for q in quadrants:
                queue.dma_start(out=plane[q:P:32].bitcast(I32), in_=rows[0, q:16:4, :].bitcast(I32))

        offs_t = held.tile([P, S // 16], U16, name="offs_t")
        pos_t = held.tile([P, J // 16], U16, name="pos_t")
        offs2_t = held.tile([P, J // 16], U16, name="offs2_t")
        tab_w = keep([P, T], U32, "tab_w")
        tab_s = keep([P, T], U8, "tab_s")
        tab2_w = keep([P, T2], U32, "tab2_w", tag="tab2_w")
        tab2_s = keep([P, T2], U8, "tab2_s")
        w8_s_raw = keep([P, H], U8, "w8_s_raw", tag="w8_s_raw")
        w4_s_raw = keep([P, H], U8, "w4_s_raw", tag="w4_s_raw")
        rows = [keep([P, 2 * P], F32, f"rows{e}") for e in range(2)]
        ident = keep([P, P], F32, "ident")

        nc.gpsimd.memset(tab_s[:].bitcast(I32), 0)
        nc.vector.memset(w4_s_raw[:].bitcast(I32), 0)
        nc.vector.memset(tab2_s[:].bitcast(I32), 0)
        nc.vector.memset(rows[0][:], 0.0)
        nc.gpsimd.memset(w8_s_raw[:].bitcast(I32), 0)
        nc.gpsimd.memset(rows[1][:], 0.0)
        make_identity(nc, ident[:])

        ws_rows = ws.rearrange("(p j) r -> p j r", j=4)
        ws_raw = [keep([P, 4, 512], F32, f"ws_raw{a}") for a in range(PASSES)]
        wo_raw = [keep([P, 4, N], F32, f"wo_raw{a}") for a in range(PASSES)]
        w8_w_raw = [keep([P, 512], I32, "w8_w_raw0", tag="w8_w_raw0")]
        w4_w_raw = keep([P, 2 * H], U8, "w4_w_raw")
        w8_rows = w8_words[0].rearrange("p c i -> p (c i)").bitcast(I32)

        by_slot = "(g t i) -> t g i"
        nc.sync.dma_start(offs_t[:], offs)
        nc.sync.dma_start(out=w4_w_raw[:].bitcast(I32), in_=w4_words[0].bitcast(I32))
        load_plane(nc.sync, tab_s[:], tab_scales, range(2))
        load_plane(nc.scalar, tab_s[:], tab_scales, range(2, 4))
        nc.sync.dma_start(out=tab_w[:].bitcast(I32), in_=tab_words[0].rearrange("p t i -> p (t i)").bitcast(I32))
        nc.sync.dma_start(offs2_t[:], offs2)
        load_plane(nc.sync, w4_s_raw[:], w4_scales)
        nc.sync.dma_start(out=ws_raw[0][:], in_=ws_rows[:, :, 0:512])
        nc.sync.dma_start(out=rows[0][0:4, :].rearrange("t (g i) -> t g i", i=8), in_=bs.rearrange(by_slot, t=4, i=8))
        load_plane(nc.sync, tab2_s[:], tab2_scales)
        nc.sync.dma_start(out=tab2_w[:].bitcast(I32), in_=tab2_words[0].rearrange("p t i -> p (t i)").bitcast(I32))
        load_plane(nc.sync, w8_s_raw[:], w8_scales)
        nc.sync.dma_start(out=w8_w_raw[0][:], in_=w8_rows[:, 0:512])
        wo_rows = wo.rearrange("(a q t i) n -> a t q i n", a=PASSES, t=4, i=8)

        def load_wo(a):
            for t in range(4):
                nc.sync.dma_start(out=wo_raw[a][:, t, :], in_=wo_rows[a, t])

        nc.sync.dma_start(out=ws_raw[1][:], in_=ws_rows[:, :, 512:1024])
        nc.sync.dma_start(pos_t[:], pos1)
        w8_late = keep([P, 512], I32, "w8_late")
        for t in range(4):
            nc.sync.dma_start(
                out=w8_late[:, P * t : P * (t + 1)].rearrange("p (q i) -> p q i", i=8),
                in_=w8_rows[:, 512:1024].rearrange("p (q t i) -> p t q i", t=4, i=8)[:, t],
            )
        load_wo(0)
        nc.sync.dma_start(out=rows[1][0:4, :].rearrange("t (g i) -> t g i", i=8), in_=gain.rearrange(by_slot, t=4, i=8))
        nc.sync.dma_start(out=rows[1][4:8, 0:P], in_=bo.rearrange("(b p) -> b p", p=P))
        load_wo(1)

        def onto_partitions(staged, name):
            turned = work_bank("P0")
            for a in range(PASSES):
                nc.tensor.transpose(turned[:, P * a : P * (a + 1)], staged[:, P * a : P * (a + 1)], ident[:])
            cols = keep([P, PASSES, 8], F32, name)
            nc.scalar.copy(out=cols[:], in_=turned[:, 0 : 2 * P].rearrange("p (a c) -> p a c", a=PASSES)[:, :, 0:8])
            return cols, turned

        bs_cols, bs_bank = onto_partitions(rows[0], "bs_cols")

        v_w = [keep([P, BANK], U32, "v_w0")]
        w4_s = keep([P, H], U8, "w4_s")
        v_s = keep([P, S], U8, "v_s")
        v2_w = keep([P, J], U32, "v2_w")
        v2_s = keep([P, J], U8, "v2_s")
        w4_w = keep([P, 2 * H], U8, "w4_w")
        w8_s = keep([P, H], U8, "w8_s")
        w8_first = keep([P, P], I32, "w8_first", tag="w8_first")
        w8_w = [keep([P, 512], I32, "w8_w0"), w8_late]
        ws_b = {}
        ws_q = {}

        def reorder(dst, src, groups, engine=nc.vector):
            engine.tensor_copy(
                out=dst.rearrange("p (a t q i) -> p a q t i", a=groups, t=4, q=16),
                in_=src.rearrange("p (a q t i) -> p a q t i", a=groups, t=4, q=16),
            )

        def round_ws(s, copy, tag=""):
            a, t = divmod(s, 4)
            if s // 2 not in ws_b:
                ws_b.update({s // 2: keep([P, 2 * 512], BF16, f"ws_b{s // 2}", tag=tag)})
            copy(
                out=ws_b[s // 2][:, 512 * (s % 2) : 512 * (s % 2 + 1)].rearrange("p (q i e j) -> p q i j e", q=16, e=4, j=4),
                in_=ws_raw[a][:].rearrange("p j (q t i e) -> p t q i j e", t=4, i=2, e=4)[:, t],
            )

        def quantize(words, plane, src):
            nc.vector.quantize_mx(out=words.bitcast(FP8X4), scales=plane, in_=src)

        def quantize_ws(s0, s1, tag=""):
            words = keep([P, P * (s1 - s0)], U32, f"ws_w{s0}", tag=tag)
            plane = keep([P, P * (s1 - s0)], U8, f"ws_s{s0}")
            quantize(words[:], plane[:], ws_b[s0 // 2][:])
            for s in range(s0, s1):
                cols = slice(P * (s - s0), P * (s - s0 + 1))
                ws_q.update({s: (words[:, cols], plane[:, cols])})

        reorder(w4_w[:].bitcast(I32), w4_w_raw[:].bitcast(I32), PASSES, nc.gpsimd)
        nc.vector.tensor_copy(out=v_s[:], in_=tab_s[:].indirect(offs_t[:]))
        nc.vector.tensor_copy(out=v_w[0][:, 0:256], in_=tab_w[:].indirect(offs_t[:, 0:16]))
        nc.vector.tensor_copy(out=v_w[0][:, 256:512], in_=tab_w[:].indirect(offs_t[:, 16:32]))
        reorder(w4_s[:].bitcast(I32), w4_s_raw[:].bitcast(I32), PASSES, nc.gpsimd)
        v_w.append(keep([P, BANK], U32, "v_w1"))
        nc.vector.tensor_copy(out=v_w[1][:], in_=tab_w[:].indirect(offs_t[:, 32:64]))
        for s in range(2):
            round_ws(s, nc.vector.tensor_copy)
        quantize_ws(0, 2)
        nc.vector.tensor_copy(out=v2_s[:], in_=tab2_s[:].indirect(offs2_t[:]))
        nc.vector.tensor_copy(out=v2_w[:], in_=tab2_w[:].indirect(offs2_t[:]))
        reorder(w8_s[:].bitcast(I32), w8_s_raw[:].bitcast(I32), PASSES, nc.gpsimd)
        by_slice = w8_w_raw[0][:].rearrange("p (q t i) -> p t q i", t=4, q=16)
        nc.gpsimd.tensor_copy(out=w8_first[:].rearrange("p (q i) -> p q i", q=16), in_=by_slice[:, 0])
        nc.gpsimd.tensor_copy(
            out=w8_w[0][:, P:512].rearrange("p (t q i) -> p q t i", t=3, q=16),
            in_=w8_w_raw[0][:].rearrange("p (q t i) -> p q t i", t=4, q=16)[:, :, 1:4, :],
        )
        for s in range(2, 4):
            round_ws(s, nc.vector.tensor_copy, tag="tab2_w")
        quantize_ws(2, 4)

        x1 = {}
        x2 = {}
        b = [keep([P, J], F32, f"b_{s}", tag=f"b_{s}") for s in range(SLICES)]
        scaled = {}
        u = [keep([P, 4, J], F32, f"u_{a}", tag=f"u_{a}") for a in range(PASSES)]

        def product(lhsT, lhsT_scale, words, plane, tag):
            bank = work_bank(tag)
            nc.tensor.matmul_mx(out=bank[:], lhsT=lhsT, lhsT_scale=lhsT_scale, rhs=words.bitcast(FP8X4), rhs_scale=plane, start=True, stop=True)
            return bank

        def make_x1(s, halves=range(2)):
            a, t = divmod(s, 4)
            if s not in x1:
                x1.update({s: keep([P, S], F32, f"x1_{s}", tag=f"x1_{s}")})
            for h in halves:
                bank = product(ws_q[s][0].bitcast(FP8X4), ws_q[s][1], v_w[h][:], v_s[:, BANK * h : BANK * (h + 1)], X1_BANKS[s][h])
                nc.scalar.activation(out=x1[s][:, BANK * h : BANK * (h + 1)], in_=bank[:], func=ACT.Identity, bias=bs_cols[:, a, t : t + 1])

        def make_b(s):
            a, t = divmod(s, 4)
            words = w8_first[:] if s == 0 else w8_w[a][:, P * t : P * (t + 1)]
            bank = product(words.bitcast(FP8X4), w8_s[:, P * s : P * (s + 1)], v2_w[:], v2_s[:], B_BANKS[s])
            (nc.vector.tensor_copy if s == 0 else nc.scalar.copy)(out=b[s][:], in_=bank[:])

        def pick_scale(s):
            scaled[s] = ring.tile([P, J], F32, name="scaled")
            nc.vector.tensor_tensor(scaled[s][:], x1[s][:].indirect(pos_t[:]), b[s][:], ALU.mult)

        def make_x2(s, halves=range(2)):
            if s not in x2:
                x2.update({s: keep([P, S], F32, f"x2_{s}", tag=f"x2_{s}" if s < 3 else f"x1_{s - 3}")})
            for h in halves:
                bank = product(w4_w[:, 2 * P * s : 2 * P * (s + 1)].bitcast(FP4X4), w4_s[:, P * s : P * (s + 1)], v_w[h][:], v_s[:, BANK * h : BANK * (h + 1)], X2_BANKS[s][h])
                nc.scalar.copy(out=x2[s][:, BANK * h : BANK * (h + 1)], in_=bank[:])

        def shift_side(s, pieces):
            a, t = divmod(s, 4)
            for j0, j1 in pieces:
                nc.vector.tensor_tensor(u[a][:, t, j0:j1], x2[s][:].indirect(pos_t[:, j0 // 16 : j1 // 16]), scaled[s][:, j0:j1], ALU.add)

        def tanh(s, j0, j1):
            a, t = divmod(s, 4)
            nc.scalar.activation(out=u[a][:, t, j0:j1], in_=u[a][:, t, j0:j1], func=ACT.Tanh)

        def tanh_pair(s):
            a, t = divmod(s, 4)
            nc.scalar.activation(out=u[a][:, t : t + 2, :], in_=u[a][:, t : t + 2, :], func=ACT.Tanh)

        def apply_gain(a, j0, j1):
            width = j1 - j0
            z_b = keep([P, 4 * width], BF16, f"z_b{a}_{j0}")
            nc.vector.tensor_tensor(
                z_b[:].rearrange("p (c i t) -> p c t i", t=4, i=4),
                u[a][:, :, j0:j1].rearrange("p t (c i) -> p c t i", i=4),
                (late_bank[:, 0:4] if a == 0 else late_cols[:, a, 0:4]).unsqueeze(1).unsqueeze(3).to_broadcast([P, width // 4, 4, 4]),
                ALU.mult,
            )
            return z_b

        def quantize_z(z_b, name, tag=""):
            width = z_b.shape[1] // 4
            z_w = keep([P, width], U32, f"z_w{name}", tag=tag)
            z_s = keep([P, width], U8, f"z_s{name}")
            quantize(z_w[:], z_s[:], z_b[:])
            return z_w, z_s

        wo_b = {}
        wo_w = keep([P, PASSES * N], U32, "wo_w")
        wo_s = keep([P, PASSES * N], U8, "wo_s")

        def round_wo(a, copy, n0=0, n1=N):
            if a not in wo_b:
                wo_b.update({a: keep([P, 4 * N], BF16, f"wo_b{a}", tag="x2_2" if a == 0 else "b_4")})
            copy(
                out=wo_b[a][:, 4 * n0 : 4 * n1].rearrange("p (c i t) -> p c t i", t=4, i=4),
                in_=wo_raw[a][:, :, n0:n1].rearrange("p t (c i) -> p c t i", i=4),
            )

        def quantize_wo(a):
            quantize(wo_w[:, N * a : N * (a + 1)], wo_s[:, N * a : N * (a + 1)], wo_b[a][:])

        def second_pass(acc, a, nt, words, plane, start, stop):
            cols = slice(N * a + P * nt, N * a + P * (nt + 1))
            nc.tensor.matmul_mx(out=acc, lhsT=(wo_w_first[:, cols] if a == 0 and P * nt < POOL_COLS else wo_w[:, cols]).bitcast(FP8X4), lhsT_scale=wo_s[:, cols], rhs=words.bitcast(FP8X4), rhs_scale=plane, start=start, stop=stop)

        out_rows = out.rearrange("(b p) j -> p b j", p=P)

        for c0, tags in ((0, ("X", "H0")), (256, ("H1", "S0"))):
            for s in range(2):
                if s not in x2:
                    x2.update({s: keep([P, S], F32, f"x2_{s}", tag=f"x2_{s}")})
                bank = work_bank(tags[s])
                nc.tensor.matmul_mx(
                    out=bank[:, 0:256], lhsT=w4_w[:, 2 * P * s : 2 * P * (s + 1)].bitcast(FP4X4), lhsT_scale=w4_s[:, P * s : P * (s + 1)],
                    rhs=v_w[0][:, c0 : c0 + 256].bitcast(FP8X4), rhs_scale=v_s[:, c0 : c0 + 256], start=True, stop=True,
                )
                nc.scalar.copy(out=x2[s][:, c0 : c0 + 256], in_=bank[:, 0:256])
        make_x2(2, [0])
        for s in range(3):
            make_x2(s, [1])
        make_x1(0)
        make_x1(1)
        make_b(0)
        for s in range(4, 6):
            round_ws(s, nc.vector.tensor_copy)
        make_b(1)
        make_b(2)
        make_b(3)
        pick_scale(0)
        pick_scale(1)
        shift_side(0, [(0, J)])
        quantize_ws(4, 6, tag="b_1")
        make_x1(2)
        pick_scale(2)
        for s in range(6, SLICES):
            round_ws(s, nc.scalar.copy, tag="b_0")
        shift_side(1, [(0, J)])
        quantize_ws(6, 8)
        make_x1(3)
        pick_scale(3)
        make_x2(3)
        shift_side(2, [(0, J)])
        round_wo(0, nc.vector.tensor_copy, POOL_COLS, N)
        shift_side(3, [(0, J)])
        quantize(wo_w[:, POOL_COLS:N], wo_s[:, POOL_COLS:N], wo_b[0][:, 4 * POOL_COLS : 4 * N])
        make_x1(4)
        make_b(4)
        pick_scale(4)
        late_cols, late_bank = onto_partitions(rows[1], "late_cols")
        for s in range(4, SLICES):
            if s + 1 < SLICES:
                make_x1(s + 1)
                make_b(s + 1)
                pick_scale(s + 1)
            if s == 4:
                make_x2(4)
                for early in range(0, 4, 2):
                    tanh_pair(early)
                shift_side(4, [(0, J)])
                z0_b = apply_gain(0, 0, J)
                wo_b_first = keep([P, 4 * POOL_COLS], BF16, "wo_b_first", tag="x1_5")
                nc.gpsimd.tensor_copy(
                    out=wo_b_first[:].rearrange("p (n t) -> p n t", t=4),
                    in_=wo_raw[0][:, :, 0:POOL_COLS].rearrange("p t n -> p n t"),
                )
            if s == 5:
                round_wo(1, nc.scalar.copy)
            if s > 4:
                make_x2(s)
            if s == SLICES - 1:
                z0 = quantize_z(z0_b, "0", tag="x1_3")
            if s == 5:
                wo_w_first = keep([P, POOL_COLS], U32, "wo_w_first", tag="u_0")
                quantize(wo_w_first[:], wo_s[:, 0:POOL_COLS], wo_b_first[:])
            if s > 4:
                shift_side(s, [(0, J)] if s + 1 < SLICES else TAIL)
            if s == 5:
                quantize_wo(1)

        def gain_on_scalar(s, j0, j1):
            a, t = divmod(s, 4)
            nc.scalar.activation(out=u[a][:, t, j0:j1], in_=u[a][:, t, j0:j1], func=ACT.Copy, scale=late_cols[:, a, t : t + 1])

        def round_z(a, j0, j1):
            z_b = keep([P, 4 * (j1 - j0)], BF16, f"z_b{a}_{j0}")
            nc.vector.tensor_copy(
                out=z_b[:].rearrange("p (c i t) -> p c t i", t=4, i=4),
                in_=u[a][:, :, j0:j1].rearrange("p t (c i) -> p c t i", i=4),
            )
            return z_b

        tanh_pair(4)
        for s in range(4, 6):
            gain_on_scalar(s, TAIL[WHOLE][0], J)
        tanh(6, 0, J)


        banks = [[work_bank(tag)] * 2 for tag in ("S0", "X", "S1")] + [[work_bank("H1"), work_bank("H0")]]

        def second_stage(a, piece, words, plane):
            split = piece == len(TAIL) - 1
            for nt in range(4):
                first = nt % 2 == 0 if split else nt == 0
                last = nt % 2 == 1 if split else nt == 3
                second_pass(banks[piece][nt // 2][:, P * nt : P * (nt + 1)], a, nt, words, plane, a == 0 and first, a == 1 and last)

        for piece, (j0, j1) in enumerate(TAIL):
            second_stage(0, piece, z0[0][:, j0:j1], z0[1][:, j0:j1])
        for piece, (j0, j1) in enumerate(TAIL):
            tanh(SLICES - 1, j0, j1)
            if piece == WHOLE - 1:
                gain_on_scalar(SLICES - 2, TAIL[WHOLE][0], J)
            if piece >= WHOLE:
                gain_on_scalar(SLICES - 1, j0, j1)
        z_b = [apply_gain(1, *TAIL[0])]
        z1 = []
        for piece in range(len(TAIL)):
            if piece + 1 < len(TAIL):
                z_b.append((apply_gain if piece + 1 < WHOLE else round_z)(1, *TAIL[piece + 1]))
            z1.append(quantize_z(z_b[piece], f"1_{piece}"))

        def add_bias(res, acc, nt):
            nc.scalar.activation(out=res, in_=acc, func=ACT.Identity, bias=late_cols[:, 0, 4 + nt : 5 + nt])

        def finish(piece, nt0, nt1, on_scalar, queue):
            j0, j1 = TAIL[piece]
            acc = banks[piece][nt0 // 2][:, P * nt0 : P * nt1].rearrange("p (e j) -> p e j", j=P)
            res = keep([P, nt1 - nt0, P], F32, f"res{piece}_{nt0}")
            if on_scalar:
                for nt in range(nt0, nt1):
                    add_bias(res[:, nt - nt0, :], acc[:, nt - nt0, :], nt)
            else:
                nc.vector.tensor_tensor(res[:], acc, late_cols[:, 0, 4 + nt0 : 4 + nt1].unsqueeze(2).to_broadcast([P, nt1 - nt0, P]), ALU.add)
            queue.dma_start(out=out_rows[:, nt0:nt1, j0:j1], in_=res[:])

        for piece in range(len(TAIL)):
            second_stage(1, piece, z1[piece][0][:], z1[piece][1][:])
            if piece < WHOLE:
                finish(piece, 0, 2, True, nc.sync)
                finish(piece, 2, 4, True, nc.sync)
            elif piece + 1 < len(TAIL):
                finish(piece, 0, 4, False, nc.sync)
            else:
                finish(piece, 0, 2, True, nc.scalar)
                finish(piece, 2, 4, False, nc.sync)
